import numpy as np, ml_dtypes
CORES = [16,17,18,19,32,33,34,35]
N = 8
BF = ml_dtypes.bfloat16
def gentries(a):
    return np.ascontiguousarray(a.reshape(8, 16, -1).transpose(0, 2, 1)).reshape(8, -1)
def gtable(e):
    e = np.asarray(e); return np.ascontiguousarray(e.reshape(8, -1, 16).transpose(0, 2, 1)).reshape(128, -1).astype(np.int32)
W, L, RO = 2048, 256, 3
NONE = W - 1
def link(rng, n, m, share):
    q, g, k, c = np.nonzero((m != NONE) & (rng.random(m.shape) < share))
    n[q, g, rng.integers(0, 16, len(q)), m[q, g, k, c]] = c
def world(rng, fill, stray, share):
    s = (N, 8, 16, W)
    m = np.where(rng.random(s) < fill, rng.integers(0, NONE, s), NONE); n = np.where(rng.random(s) < stray, rng.integers(0, NONE, s), NONE)
    link(rng, n, m, share)
    return n, m
def words(rng):
    pool = rng.integers(0, NONE, (N, 8, 40)); a = np.take_along_axis(pool, rng.integers(0, 40, (N, 8, L)), 2)
    return np.where(rng.random((N, 8, L)) < 0.5, a, rng.integers(0, NONE, (N, 8, L)))
def pack(x, n, m, w, z, th):
    x[..., NONE] = 255; n[..., NONE] = NONE; m[..., NONE] = NONE
    return {"x": x.reshape(N, 128, W).astype(np.float32).astype(BF), "nm": np.ascontiguousarray((n + 4096 * m).reshape(N, 128, W)).astype(np.int32),
            "w": np.stack([gtable(a) for a in w]), "z": z.reshape(N, 128, L).astype(np.float32).astype(BF),
            "th": np.repeat(th, 16, axis=1).reshape(N, 128, 1).astype(np.int32)}
def setup_inputs(rng):
    n, m = world(rng, rng.choice(np.array([0.0, 0.1, 0.4, 0.8, 1.0]), (N, 8, 1, W)), 0.3, 0.75)
    return pack(rng.integers(0, 16, (N, 8, 16, W)), n, m, words(rng), rng.integers(0, 16, (N, 8, 16, L)), rng.integers(55, 86, (N, 8)))
def setup_inputs_crowd(rng):
    n, m = world(rng, 0.7, 0.3, 0.7); x = rng.integers(0, 16, (N, 8, 16, W)); z = rng.integers(0, 16, (N, 8, 16, L)); w = np.zeros((N, 8, L), np.int64)
    for g in range(8):
        pw = rng.permutation(NONE)[:12]; po = rng.permutation(NONE)[:6]
        for q in range(N):
            mm = po[rng.integers(0, 6, (16, 12))]; mm[rng.random((16, 12)) < 0.3] = NONE; mm[:, 0] = NONE; mm[0, 0] = po[0]
            m[q, g][:, pw] = mm; n[q, g][:, po] = NONE
            k, c = np.nonzero(mm != NONE); n[q, g][rng.integers(0, 16, len(k)), mm[k, c]] = pw[c]
            n[q, g][0, po[0]] = pw[0]
            v = int(rng.integers(1, 13)); w[q, g] = pw[rng.integers(0, v, L)]; w[q, g, 0] = pw[0]; w[q, g, L - 1] = pw[0]
            near = np.clip(x[q, g][:, po[rng.integers(0, 6, L)]] + rng.integers(-1, 2, (16, L)), 0, 15)
            z[q, g] = np.where(rng.random(L) < 0.5, near, z[q, g])
            a = x[q, g][:, po[0]].copy(); far = np.where(a < 8, 15, 0)
            z[q, g][:, 0] = far if g % 2 == 0 else a
            z[q, g][:, L - 1] = a if g % 2 == 0 else far
    return pack(x, n, m, w, z, rng.integers(20, 91, (N, 8)))
def setup_inputs_ties(rng):
    proto = rng.integers(0, 12, (8, 16, 4)); kind = rng.integers(0, 4, (N, 8, W))
    x = np.stack([np.take_along_axis(proto, kind[q][:, None, :], 2) for q in range(N)])
    m = np.take_along_axis(rng.integers(0, NONE, (N, 8, 4, W)), rng.integers(0, 4, (N, 8, 16, W)), 2)
    n = np.full((N, 8, 16, W), NONE, np.int64); link(rng, n, m, 0.6)
    w = words(rng); one = np.take_along_axis(m, w[:, :, None, :], 3)[:, :, :1]
    z = np.take_along_axis(x, one, 3) + 2; z[:, :, 0] += rng.integers(-1, 2, (N, 8, L))
    return pack(x, n, m, w, z, np.full((N, 8), 32, np.int64))
def setup_inputs_hollow(rng):
    n, m = world(rng, 0.6, 0.2, 0.7); w = words(rng)
    n[:, 0::4] = NONE
    for g in (0, 4):
        o = rng.permutation(NONE); a, b = o[:L // 2], o[L // 2:]
        for q in range(N):
            if q % 2 == 0:
                m[q, g][:, a] = NONE; w[q, g, rng.permutation(L)[:L // 2]] = a
            else:
                m[q, g][:, a] = rng.integers(0, NONE, (16, L // 2))
                w[q, g] = np.where(rng.random(L) < 0.5, b[rng.integers(0, 40, L)], b[rng.integers(0, len(b), L)])
    m[:, 1::4] = np.where(rng.random((N, 2, 1, W)) < 0.8, NONE, m[:, 1::4])
    m[:, 2::4] = np.where(rng.random((N, 2, 16, W)) < 0.9, NONE, m[:, 2::4]); n[:, 2::4] = np.where(rng.random((N, 2, 16, W)) < 0.8, rng.integers(0, NONE, (N, 2, 16, W)), n[:, 2::4])
    for c in (0, NONE - 1):
        m[:, 3::4, :, c] = rng.choice(np.array([0, NONE - 1, NONE]), (N, 2, 16)); n[:, 3::4, :, c] = rng.choice(np.array([0, NONE - 1, NONE]), (N, 2, 16))
    w[:, 3::4] = rng.choice(np.array([0, NONE - 1]), (N, 2, L))
    return pack(rng.integers(0, 16, (N, 8, 16, W)), n, m, w, rng.integers(0, 16, (N, 8, 16, L)), rng.choice(np.array([0, 1, 90, 255]), (N, 8)))
def setup_inputs_mutual(rng):
    n = np.full((N, 8, 16, W), NONE, np.int64); m = np.full((N, 8, 16, W), NONE, np.int64); i = np.arange(NONE)[None, :]
    for q in range(N):
        for g in range(8):
            ob = rng.permutation(NONE); wo = rng.permutation(NONE); s = rng.permutation(NONE)[:16]; s2 = rng.permutation(s)
            m[q, g][:, wo] = ob[(i + s[:, None]) % NONE]; n[q, g][:, ob] = wo[(i - s2[:, None]) % NONE]
    th = rng.integers(40, 80, (N, 8)); th[:, ::2] = 255
    x = rng.integers(0, 16, (N, 8, 16, W)); w = words(rng); z = rng.integers(0, 16, (N, 8, 16, L))
    r = int(rng.integers(0, N)); r1, r2, r3 = (r - 1) % N, (r - 2) % N, (r - 3) % N
    th[r] = rng.permutation(np.array([241, 244, 247, 250, 253, 254, 255, 255])); won = int(rng.integers(3, 16)); h = int(rng.integers(0, 8))
    for g in range(8):
        pw = rng.permutation(np.setdiff1d(np.arange(NONE), w[[r, r1, r2], g]))[:33]; ob = rng.permutation(NONE)[:33]; tb = rng.permutation(NONE)[:32]
        m[r, g][np.isin(m[r, g], ob)] = NONE; m[r, g][:, pw] = ob; n[r, g][0::2][:, ob] = pw; x[r, g][:, ob] = 15
        m[r2, g][np.isin(m[r2, g], tb)] = NONE; m[r2, g][:, pw[:32]] = tb; n[r2, g][:, tb] = pw[:32]
        x[r2, g][:, tb] = (np.arange(32)[None, :] + rng.permutation(16)[:, None]) // 16
        p = rng.permutation(L); w[r1, g, p[:32]] = pw[:32]; w[r3, g, rng.permutation(L)[:32]] = pw[:32]
        if g == h: w[r1, g, p[32:32 + won]] = pw[32]
        m[r1, g][:, w[r1, g]] = NONE; m[r3, g][:, pw[:32]] = NONE
        if g == h:
            c = int(rng.integers(0, NONE)); m[r1, g][:, pw[32]] = c; n[r1, g][:, c] = pw[32]
    return pack(x, n, m, w, z, th)
def setup_inputs_spread(rng):
    n, m = world(rng, rng.random((N, 8, 1, W)), rng.random((N, 8, 1, W)), 0.7)
    x = rng.integers(0, 16, (N, 8, 16, W)) >> rng.integers(0, 5, (N, 8, 1, W)); z = rng.integers(0, 16, (N, 8, 16, L)) >> rng.integers(0, 5, (N, 8, 1, L))
    th = rng.integers(0, 256, (N, 8)); th[0, 0] = 0; th[1, 1] = 255
    return pack(x, n, m, words(rng), z, th)
def check_inputs(d):
    bad = []; x = np.asarray(d["x"]).astype(np.float32); z = np.asarray(d["z"]).astype(np.float32); p = np.asarray(d["nm"]).astype(np.int64); th = np.asarray(d["th"])
    if not np.all((x[..., :NONE] >= 0) & (x[..., :NONE] <= 15) & (np.floor(x[..., :NONE]) == x[..., :NONE])): bad.append("range of x")
    if not np.all(x[..., NONE] == 255): bad.append("last column of x")
    if not np.all((p >= 0) & ((p & 4095) <= NONE) & ((p >> 12) <= NONE)): bad.append("range of nm")
    if not np.all(p[..., NONE] == NONE + 4096 * NONE): bad.append("last column of nm")
    if np.min(d["w"]) < 0 or np.max(d["w"]) > NONE - 1: bad.append("range of w")
    if not np.all((z >= 0) & (z <= 15) & (np.floor(z) == z)): bad.append("range of z")
    if np.min(th) < 0 or np.max(th) > 255: bad.append("range of th")
    if not np.all(th.reshape(N, 8, 16) == th.reshape(N, 8, 16)[:, :, :1]): bad.append("th alike in a group")
    return bad
def reference(x, nm, w, z, th):
    X = x.astype(np.float32).astype(np.int32).reshape(N, 8, 16, W); P = nm.astype(np.int32).reshape(N, 8, 16, W); NA = P & 4095; MA = P >> 12
    wl = np.stack([gentries(a) for a in w]).astype(np.int32); zl = z.astype(np.float32).astype(np.int32).reshape(N, 8, 16, L)
    t0 = th.astype(np.int32).reshape(N, 8, 16)[:, :, :1]; wins = [0] * N
    lane = np.arange(L); earlier = lane[None, :] < lane[:, None]; rows = np.arange(16)[:, None]
    for t in range(RO):
        nw, nz, cnt = [], [], []
        for a in range(N):
            n, m, xx, ww, zz = NA[a], MA[a], X[a], wl[a], zl[a]
            e = np.take_along_axis(m, ww[:, None, :], 2); ef = e.reshape(8, 1, 16 * L)
            D = np.add.reduce(np.abs(zz[:, :, None, :] - np.take_along_axis(xx, ef, 2).reshape(8, 16, 16, L)), axis=1)
            real = np.any(np.take_along_axis(n, ef, 2).reshape(8, 16, 16, L) == ww[:, None, None, :], axis=1)
            key = np.where(real, D, D + 8192); k = np.argmin(key, axis=1)[:, None, :]
            o = np.take_along_axis(e, k, 1)[:, 0]; hit = np.take_along_axis(key, k, 1)[:, 0] < t0[a] + (wins[a] & 31)
            no = np.take_along_axis(n, o[:, None, :], 2); xo = np.take_along_axis(xx, o[:, None, :], 2)
            mn = np.take_along_axis(m, no.reshape(8, 1, 16 * L), 2).reshape(8, 16, 16, L)
            cand = np.any(mn == o[:, None, None, :], axis=1) & (no != NONE)
            few = np.where(cand, np.add.reduce((mn != NONE).astype(np.int32), axis=1), 17); j = np.argmin(few, axis=1)[:, None, :]
            nw.append(np.where(np.any(cand, axis=1), np.take_along_axis(no, j, 1)[:, 0], ww)); nz.append(xo); cnt.append(int(np.count_nonzero(hit)))
            h = hit[:, None, :]
            n2 = np.where(h, np.where(no == ww[:, None, :], no, NONE), np.where(rows == ((lane + t) & 15), ww[:, None, :], no))
            x2 = np.where(h, xo, xo + np.clip(zz - xo, -2, 2)); m2 = np.where(e == o[:, None, :], e, NONE)
            go = ~np.any((o[:, :, None] == o[:, None, :]) & earlier, axis=2) & (o != NONE)
            gw = ~np.any((ww[:, :, None] == ww[:, None, :]) & earlier, axis=2) & hit
            for g in range(8):
                c = o[g][go[g]]; n[g][:, c] = n2[g][:, go[g]]; xx[g][:, c] = x2[g][:, go[g]]
                m[g][:, ww[g][gw[g]]] = m2[g][:, gw[g]]
        d = 1 + t % (N - 1); wins = cnt
        wl = np.stack([nw[(a - d) % N] for a in range(N)]).astype(np.int32); zl = np.stack([nz[(a - d) % N] for a in range(N)])
    return {"ynm": (NA + 4096 * MA).reshape(N, 128, W).astype(np.float32), "yw": np.stack([gtable(a) for a in wl]).astype(np.float32), "yz": zl.reshape(N, 128, L).astype(np.float32).astype(BF)}

@@ -1,0 +1,612 @@
+from concourse.mybir import AluOpType, AxisListType, ActivationFunctionType
+
+ALU = AluOpType
+ACT = ActivationFunctionType
+RO, NR, W, NONE = 3, 8, 2048, 2047
+H = 2
+REP = 4
+XV = ((), (3,))
+TRIES = 1500
+SPEEDS = [(1.5, 3.8, 0.42, 110.0), (1.1, 2.0, 0.42, 110.0), (2.0, 5.5, 0.42, 160.0), (1.5, 3.8, 0.6, 200.0)]
+NB = 16 // H
+LH = 16 * NB
+EW = LH + 32
+TW = 2 * LH + 32
+ZW = LH + NB
+WP = W + 32
+F32, BF, F16, I32, U16 = "float32", "bfloat16", "float16", "int32", "uint16"
+
+SCRATCH = {_n: ("sbuf", [128, _c], _d) for _n, _c, _d in [
+    ("nmi", W, I32), ("NI", W, I32), ("NT", WP, F32), ("MT", WP, F32), ("MC", WP, F32), ("XT", WP, BF),
+    ("zin", 256, BF), ("thi", 4, I32), ("col", 32, F32), ("coli", 32, I32),
+    ("ones", 2304, BF), ("m4", 2304, BF), ("Sel", 2048, BF), ("Bm", 2304, BF), ("Bt", 2304, BF), ("Bu", 2304, BF),
+    ("B1", 144, BF), ("B15", 144, BF), ("B0", 144, BF), ("Bn", 144, BF),
+    ("Id", 128, BF), ("nId", 128, BF), ("I12", 128, BF), ("I23", 128, BF), ("I24", 128, BF), ("I34", 128, BF),
+    ("If", 128, F32), ("nIf", 128, F32), ("KC", 256, BF), ("iC", 16, F32), ("pm", 16, U16), ("cN", 32, F32),
+    ("wu", 16, U16), ("ou", 16, U16), ("wl", 32, F16), ("LST", 80, F16), ("thr", 16, F32),
+    ("KEY", 16, I32), ("oi", 16, I32), ("KEY2", 16, I32), ("wand", 16, I32),
+    ("EP", H * EW, F32), ("NP", H * EW, F32), ("TE", H * TW, F32), ("TN", H * TW, F32),
+    ("eoff", 256, U16), ("uoff", 256, U16), ("ETf", 256, F32), ("UTf", 256, F32),
+    ("WR", REP * 256, F32), ("OR", REP * 256, F32), ("FR", 256, BF),
+    ("EQN", 4096, BF), ("XG", 4096, BF), ("AD", 4096, BF), ("EQM", 4096, BF), ("CN", 4096, BF),
+    ("SG", 256, BF), ("SG2", 256, BF), ("RUN", 64 * H, F32), ("RUN2", 64 * H, F32), ("FB", 64 * H, F32),
+    ("TR", 64 * H, F32), ("TR2", 64 * H, F32),
+    ("EQw", 512, BF), ("EQo", 512, BF), ("woff", 16, U16), ("ooff", 16, U16),
+    ("tA", 512, BF), ("sB", 512, BF), ("rM", 256, F32), ("rN", 256, F32), ("Q", 256, F32),
+    ("Mo", 256, F32), ("dM", 256, F32), ("Yw", 256, F32), ("rX", 512, BF), ("x2", 256, BF),
+    ("WI0", 16, I32), ("WI1", 16, I32), ("WI2", 16, I32), ("WF", 16, F32),
+    ("WO0", 16, I32), ("WO1", 16, I32), ("WOF", 16, F32),
+    ("ZB0", H * ZW, BF), ("ZB1", H * ZW, BF), ("ZB2", H * ZW, BF), ("ZF", 256, BF),
+    ("ZO0", H * ZW, BF), ("ZO1", H * ZW, BF), ("ZO2", H * ZW, BF)]}
+for _i in range(8):
+    SCRATCH["ps%d" % _i] = ("psum", [128, 512], F32)
+
+CYC = 0.83
+
+
+def S(name, a, b, st=1):
+    return (name, a, b, st)
+
+
+def _n(s):
+    return (s[2] - s[1] + s[3] - 1) // s[3]
+
+
+def _two(*ss):
+    return all(len(s) == 4 and s[0][0] != "@" and SCRATCH[s[0]][2] not in (F32, I32) for s in ss)
+
+
+def build_ops():
+    ops, nreg, at = [], [0], ["", 0]
+
+    def reg():
+        nreg[0] += 1
+        return "@%d" % nreg[0]
+
+    def add(eng, cost, rd, wr, fn, lat=0.0, kind="c", tag="", ge=0, se=0):
+        ops.append({"eng": eng, "fix": cost, "ge": ge, "se": se, "rd": rd, "wr": wr, "fn": fn, "lat": lat, "kind": kind,
+                    "tag": (tag or (wr or rd)[0][0]) + at[0], "t": at[1]})
+        return ops[-1]
+
+    def opnd(R, s):
+        if not isinstance(s, tuple):
+            return s
+        return R(s[0]).indirect(R(s[1])) if len(s) == 2 else R(s)
+
+    def flat(*ss):
+        out = []
+        for s in ss:
+            if isinstance(s, tuple):
+                out += list(s) if len(s) == 2 else [s]
+        return out
+
+    def vec(out, ins, per, fn, tag):
+        if len(out) == 2:
+            add("V", 50, [out[1]] + flat(*ins), [out[0]], fn, tag=tag, se=_n(ins[0]))
+        elif len(ins[0]) == 2:
+            add("V", 50, flat(*ins), [out], fn, tag=tag, ge=_n(out))
+        else:
+            add("V", max(64, per * _n(ins[0])) * CYC, flat(*ins), [out], fn, tag=tag)
+
+    def vcopy(out, in_, tag=""):
+        vec(out, [in_], 0.5 if _two(out, in_) else 1, lambda q, R: q.tensor_copy(opnd(R, out), opnd(R, in_)), tag)
+
+    def vts(out, in_, s1, s2, o0, o1=None, tag=""):
+        more = [] if o1 is None else [o1]
+        vec(out, [in_, s1, s2], 0.5 if _two(out, in_) else 1,
+            lambda q, R: q.tensor_scalar(R(out), opnd(R, in_), opnd(R, s1), opnd(R, s2), o0, *more), tag)
+
+    def vtt(out, a, b, op, tag=""):
+        vec(out, [a, b], 1 if a[0][0] == "@" or b[0][0] == "@" else 2,
+            lambda q, R: q.tensor_tensor(opnd(R, out), opnd(R, a), R(b), op), tag)
+
+    def vset(out, c):
+        add("V", max(64, _n(out) * (0.5 if _two(out) else 1)) * CYC, [], [out], lambda q, R: q.memset(R(out), c))
+
+    def vtr(out, in_):
+        vec(out, [in_], 1, lambda q, R: q.transpose(R(out), R(in_)), "")
+
+    def act(out, in_, f, bias=0.0, scale=1.0, tag=""):
+        ind = len(in_) == 2
+        add("S", 65 + (0 if ind else CYC * _n(out)), flat(in_, bias, scale), [out],
+            lambda q, R: q.activation(R(out), opnd(R, in_), f, opnd(R, bias), opnd(R, scale)), tag=tag, ge=_n(out) if ind else 0)
+
+    def mm(lst, start=True, stop=True, each=False, tag=""):
+        c = sum(max(64, _n(r)) * (4 if SCRATCH[r[0]][2] == F32 else 1) for o, l, r in lst)
+
+        def fn(q, R):
+            ins = None
+            for i, (o, l, r) in enumerate(lst):
+                ins = q.matmul(R(o), R(l), R(r), each or (start and i == 0), each or (stop and i == len(lst) - 1))
+            return ins
+        add("P", c + 64, [x[1] for x in lst] + [x[2] for x in lst], [x[0] for x in lst], fn, tag=tag)
+
+    def gsel(out, in_, pat, op, base, cm):
+        add("G", 170 + 2 * CYC * _n(out), [in_], [out],
+            lambda q, R: q.affine_select(R(out), R(in_), pat, op, 0.0, base, cm))
+
+    def giota(out, pat, base, cm):
+        kw = {} if SCRATCH[out[0]][2] == I32 else {"allow_small_or_imprecise_dtypes": True}
+        add("G", 130 + 2 * CYC * _n(out), [], [out], lambda q, R: q.iota(R(out), pat, base, cm, **kw))
+
+    def dma(eng, out, in_, lat, acc=False):
+        kw = {"accum_op": ALU.add} if acc else {}
+        add(eng, 1000 if acc else 60, [in_], [out], lambda q, R: q.dma_start(R(out), R(in_), **kw), lat=1900 + lat, kind="d")
+
+    def send(dst, src, nbytes):
+        add("G", 300, [src], [], None, lat=2200 + nbytes / 100.0, kind="r").update({"dst": dst, "src": src})
+
+    col = lambda j: S("col", j, j + 1)
+    ci = lambda j: S("coli", j, j + 1)
+    idn = lambda n, a=0: S(n, 128 * a, 128 * a + 128)
+    Bw = lambda n, a: S(n, 15 - a, 143 - a)
+    NTw, MTw, XTw = S("NT", 0, W), S("MT", 0, W), S("XT", 0, W)
+    BIG = 1.5 * 2.0 ** 35
+    AND, SHR = ALU.bitwise_and, ALU.arith_shift_right
+
+    dma("Y", S("WI0", 0, 16), S("w", 0, 0), 100)
+    for c in range(4):
+        dma("Y", S("nmi", 512 * c, 512 * c + 512), S("nm", 512 * c, 512 * c + 512), 870 * (c + 1))
+    dma("Y", S("zin", 0, 256), S("z", 0, 0), 3600)
+    dma("Y", XTw, S("x", 0, 0), 5200)
+    dma("Y", S("thi", 0, 1), S("th", 0, 0), 5200)
+    giota(ci(0), [[0, 1]], 0, 1)
+    vset(S("ones", 0, 2304), 1.0)
+    gsel(idn("Id"), idn("ones"), [[-1, 128]], ALU.is_equal, 0, 1)
+    gsel(S("Sel", 0, 2048), S("ones", 0, 2048), [[-1, 16], [-16, 8], [0, 16]], ALU.is_equal, 0, 1)
+    giota(S("iC", 0, NB), [[16 // NB, NB]], 0, 0)
+    gsel(S("B0", 0, 144), S("ones", 0, 144), [[-16, 9], [256, 16]], ALU.is_ge, -256 * 15, 1)
+    gsel(S("B1", 0, 144), S("B0", 0, 144), [[16, 9], [0, 16]], ALU.is_ge, 15, -1)
+    giota(S("KC", 0, LH), [[2048, 16], [0, NB]], 0, 0)
+    act(S("m4", 0, 2304), S("ones", 0, 2304), ACT.Copy, 0.0, -4096.0)
+    gsel(S("Bm", 0, 2304), S("m4", 0, 2304), [[-1, 16], [-16, 9], [256, 16]], ALU.is_equal, -256 * 15, 1)
+    gsel(S("Bu", 0, 2304), S("m4", 0, 2304), [[0, 16], [-16, 9], [256, 16]], ALU.is_ge, -256 * 15, 1)
+    gsel(S("Bt", 0, 2304), S("Bu", 0, 2304), [[1, 16], [16, 9], [0, 16]], ALU.is_ge, -1, -1)
+    act(S("B15", 0, 144), S("B1", 0, 144), ACT.Copy, 0.0, 32768.0)
+    act(S("Bn", 0, 144), S("B1", 0, 144), ACT.Copy, 0.0, -4096.0)
+    for n, v in (("nId", -1.0), ("I12", 4096.0), ("I23", 2.0 ** 23), ("I24", -2.0 ** 24), ("I34", -2.0 ** 34),
+                 ("If", 1.0), ("nIf", -1.0)):
+        act(idn(n), idn("Id"), ACT.Copy, 0.0, v)
+    vts(ci(1), ci(0), 15, None, AND)
+    vts(ci(2), ci(0), 4, 1, SHR, AND)
+    vts(ci(3), ci(0), NB - 2, None, AND)
+    vts(ci(4), ci(0), 1, None, AND)
+    vts(ci(5), ci(0), {16: 4, 8: 3}[NB], 16 // NB - 1, SHR, AND)
+    vcopy(S("col", 1, 6), S("coli", 1, 6))
+    vts(col(6), col(4), col(2), None, ALU.not_equal)
+    vts(col(7), col(2), -32.0, float(LH + 32), ALU.mult, ALU.add)
+    vts(col(8), col(3), col(2), 16.0, ALU.add, ALU.mult)
+    vts(col(9), col(6), col(7), col(5), ALU.mult, ALU.add)
+    vts(S("pm", 0, NB), S("iC", 0, NB), col(8), col(9), ALU.add, ALU.add)
+    vts(col(15), col(1), -1.0, -float(W), ALU.mult, ALU.add)
+    vts(col(16), col(1), -1.0, -float(W + 16), ALU.mult, ALU.add)
+    vset(S("EP", 0, H * EW), 0.0)
+    vset(S("NP", 0, H * EW), 0.0)
+    vset(S("FB", 0, 64 * H), 2.0 ** 24)
+    vset(S("cN", 0, 32), 4096.0 * NONE)
+    vts(S("wl", 0, 1), col(1), 0.0, -1.0, ALU.mult, ALU.add)
+    vts(S("LST", 0, 1), col(1), 0.0, -1.0, ALU.mult, ALU.add)
+    vts(col(11), S("thi", 0, 1), -512.0, None, ALU.add)
+    vts(col(12), col(11), 32768.0, None, ALU.mult)
+    for c in range(4):
+        a, b = 512 * c, 512 * c + 512
+        vts(S("NI", a, b), S("nmi", a, b), 4095, None, AND)
+        vts(S("MT", a, b), S("nmi", a, b), BIG, -BIG, ALU.add, ALU.add)
+        vcopy(S("NT", a, b), S("NI", a, b))
+    vset(S("MT", NONE, W), 4096.0 * W)
+    vset(S("XT", NONE, W), 40.0)
+    for h in range(H):
+        act(S("ZB0", h * ZW, h * ZW + LH), S("zin", h * LH, h * LH + LH), ACT.Identity, 31.0, -1.0)
+        vset(S("ZB0", h * ZW + LH, h * ZW + ZW), 0.0)
+
+    ep = lambda n, h: S(n, h * EW + 16, h * EW + 16 + LH)
+    row = lambda n, h, r=0: S(n, (h * REP + r) * LH, (h * REP + r + 1) * LH)
+
+    def bcast(ps, src, width, tag):
+        mm([(S(ps, a, width, 16), idn("Sel", a), src) for a in range(16)], each=True, tag=tag)
+
+    def turn(h, pad, tr, off, tf, scale):
+        e0, t0 = h * EW, h * TW
+        vtr(S(tr, t0, t0 + LH), ep(pad, h))
+        vtr(S(tr, t0 + LH, t0 + TW), S(pad, e0, e0 + EW))
+        win = (S(tr, t0, t0 + TW), S("pm", 0, NB))
+        vts(S(off, h * LH, h * LH + LH), win, scale, None, ALU.mult)
+        act(S(tf, h * LH, h * LH + LH), win, ACT.Copy, 0.0, scale)
+
+    def keys(h, eq, val, sg, tf, run, tr, first, key):
+        for c in range(LH // 64):
+            d0, k0, u = h * 16 * LH + 1024 * c, h * LH + 64 * c, val + str(c)
+            pc, pk = S(reg(), 0, 64), S(reg(), 0, 64)
+            mm([(pc, Bw("B1", a), S(eq, d0 + a, d0 + 1024, 16)) for a in range(16)], tag="C" + u)
+            act(S(sg, k0, k0 + 64), pc, ACT.Sign)
+            mm([(pk, idn("Id"), S("KC", 64 * c, 64 * c + 64)), (pk, idn("If"), S(tf, k0, k0 + 64))]
+               + [(pk, Bw("B15", a), S(val, d0 + a, d0 + 1024, 16)) for a in range(16)], stop=False, tag="K" + u)
+            mm([(pk, idn("I24"), S(sg, k0, k0 + 64))], start=False, tag="L" + val)
+            r = S(run, 64 * h, 64 * h + 64)
+            if c == 0 and first is None:
+                vts(r, pk, 2.0 ** 24 - 1, None, ALU.min)
+            else:
+                vtt(r, pk, r if c else first, ALU.min)
+        n, src, a, to = 32, run, 64 * h, 64 * h
+        while n >= NB:
+            vtt(key if n == NB else S(tr, to, to + n), S(src, a, a + n), S(src, a + n, a + 2 * n), ALU.min, tag=run)
+            src, a, to, n = tr, to, to + n, n // 2
+
+    def firsts(lst, rw, scale, eq, off, more):
+        pd, pr = reg(), S(reg(), 0, 16)
+        mm([(S(pd, a, 272, 16), idn(scale), S(lst, 0, 17)) for a in range(16)], each=True, tag="d" + eq)
+        for h in range(H):
+            for d in range(2):
+                vtt(S(eq, 256 * d + h * LH, 256 * d + h * LH + LH), S(pd, 16 - 16 * d + h * LH, 16 - 16 * d + h * LH + LH),
+                    row(rw, h), ALU.is_equal)
+        mm([(pr, idn("nId"), S(lst, 1, 17))] + [(S(pr[0], h * NB, h * NB + NB), idn("nId"), x) for h, x in enumerate(more)]
+           + [(pr, S("Bt", 143 * a + 15, 143 * a + 143), S(eq, a, 256, 16)) for a in range(16)]
+           + [(pr, Bw("Bn", a), S(eq, 256 + a, 512, 16)) for a in range(16)], tag="r" + eq)
+        for u in range(2):
+            vts(S(off, u, 16, 2), S(pr[0], u, 16, 2), col(15 + u), -1.0, ALU.max, ALU.mult)
+
+    for t in range(RO):
+        last = t == RO - 1
+        at[1] = t
+        WI, ZB, ZO = "WI%d" % t, "ZB%d" % t, "ZO%d" % t
+        if last:
+            dma("Y", S("MC", 0, W), NTw, 3500)
+            dma("G", S("MC", 0, W), MTw, 5000, acc=True)
+            vset(S("MC", NONE, W), 4097.0 * NONE)
+        for h in range(H):
+            at[0] = "." + str(h)
+            b0, b1, l0, d0, r0 = h * NB, h * NB + NB, h * LH, h * 16 * LH, h * REP * LH
+            zb = S(ZB, h * ZW, h * ZW + LH)
+            vcopy(S("wu", b0, b1), S(WI, b0, b1))
+            vcopy(S("wl", 1 + b0, 1 + b1), S(WI, b0, b1))
+            if t:
+                vcopy(ep("EP", h), (MTw, S("wu", b0, b1)))
+            else:
+                vts(ep("EP", h), (S("nmi", 0, W), S("wu", b0, b1)), BIG, -BIG, ALU.add, ALU.add)
+            turn(h, "EP", "TE", "eoff", "ETf", 1.0 / 4096)
+            p = reg()
+            bcast(p, S("wl", 1 + b0, 1 + b1), LH, "bw")
+            for r in range(REP):
+                act(row("WR", h, r), S(p, 0, LH), ACT.Copy)
+            act(S("thr", b0, b1), S(ZB, h * ZW + LH, h * ZW + ZW), ACT.Identity, col(12), -8192.0)
+            vts(S("FB", 64 * h, 64 * h + NB), S(WI, b0, b1), -2.0 ** 23, None, ALU.add)
+            for k in range(0, 16, REP):
+                vtt(S("EQN", d0 + k * LH, d0 + (k + REP) * LH),
+                    (NTw if t else S("NI", 0, W), S("eoff", l0 + k * NB, l0 + (k + REP) * NB)),
+                    S("WR", r0, r0 + REP * LH), ALU.is_equal, tag="EQN%d" % (k * NB // 64))
+            kp = 512 // LH
+            for c in range(16 // kp):
+                xg, ad = S("XG", d0 + 512 * c, d0 + 512 * c + 512), S("AD", d0 + 512 * c, d0 + 512 * c + 512)
+                if c in XV[h]:
+                    for k in range(kp):
+                        o0 = l0 + (c * kp + k) * NB
+                        vtt(S("XG", xg[1] + k * LH, xg[1] + k * LH + LH), (XTw, S("eoff", o0, o0 + NB)), zb, ALU.add, tag="xV")
+                    act(ad, xg, ACT.Abs, -31.0, tag="AD%d" % c)
+                else:
+                    act(xg, (XTw, S("eoff", l0 + 32 * c, l0 + 32 * c + 32)), ACT.Copy, tag="xS%d" % c)
+                    p = reg()
+                    mm([(S(p, 0, 512), idn("Id"), xg)] + [(S(p, k * LH, k * LH + LH), idn("Id"), zb) for k in range(kp)], tag="xP")
+                    act(ad, S(p, 0, 512), ACT.Abs, -31.0, tag="AD%d" % c)
+            keys(h, "EQN", "AD", "SG", "ETf", "RUN", "TR", None, S("KEY", b0, b1))
+            vts(S("oi", b0, b1), S("KEY", b0, b1), NONE, None, AND)
+            vcopy(S("ou", b0, b1), S("oi", b0, b1))
+            vcopy(S("LST", 1 + b0, 1 + b1), S("oi", b0, b1), tag="ol")
+            vtt(S("LST", 32 + b0, 32 + b1), S("KEY", b0, b1), S("thr", b0, b1), ALU.is_ge, tag="fail")
+            vts(S(ZO, h * ZW + LH, h * ZW + ZW), S("oi", b0, b1), float(NONE), 4096.0, ALU.is_equal, ALU.mult, tag="FL")
+        at[0] = ""
+        if last:
+            vset(S("XT", NONE, W), 255.0)
+        firsts("wl", "WR", "Id", "EQw", "woff", [])
+        for h in range(H):
+            at[0] = "." + str(h)
+            b0, b1, l0, d0, r0 = h * NB, h * NB + NB, h * LH, h * 16 * LH, h * REP * LH
+            zo = S(ZO, h * ZW, h * ZW + LH)
+            vcopy(ep("NP", h), (NTw, S("ou", b0, b1)))
+            turn(h, "NP", "TN", "uoff", "UTf", 1.0)
+            p = reg()
+            bcast(p, S("LST", 1 + b0, 1 + b1), LH, "bo")
+            for r in range(REP):
+                act(row("OR", h, r), S(p, 0, LH), ACT.Copy, 0.0, 4096.0)
+            if last:
+                act(zo, (XTw, S("ou", b0, b1)), ACT.Copy, tag="xo")
+                send(S("ZF", l0, l0 + LH), zo, 256 * LH)
+            else:
+                act(zo, (XTw, S("ou", b0, b1)), ACT.Relu, 31.0, -1.0, tag="xo")
+                send(S("ZB%d" % (t + 1), h * ZW, h * ZW + ZW), S(ZO, h * ZW, h * ZW + ZW), 256 * ZW)
+            for k in range(0, 16, REP):
+                vtt(S("EQM", d0 + k * LH, d0 + (k + REP) * LH), (MTw, S("uoff", l0 + k * NB, l0 + (k + REP) * NB)),
+                    S("OR", r0, r0 + REP * LH), ALU.is_equal, tag="EQM%d" % (k * NB // 64))
+            for c in range(LH // 32):
+                act(S("CN", d0 + 512 * c, d0 + 512 * c + 512), (MTw, S("uoff", l0 + 32 * c, l0 + 32 * c + 32)),
+                    ACT.Sign, 4096.0 * NONE, -1.0, tag="CN%d" % (c // 2))
+            keys(h, "EQM", "CN", "SG2", "UTf", "RUN2", "TR2", S("FB", 64 * h, 64 * h + 64), S("KEY2", b0, b1))
+            if last:
+                vts(S("wand", b0, b1), S("KEY2", b0, b1), NONE, None, AND)
+                vcopy(S("WOF", b0, b1), S("wand", b0, b1))
+                send(S("WF", b0, b1), S("WOF", b0, b1), 512 * NB)
+            else:
+                vts(S("WO%d" % t, b0, b1), S("KEY2", b0, b1), NONE, None, AND, tag="wand")
+                send(S("WI%d" % (t + 1), b0, b1), S("WO%d" % t, b0, b1), 512 * NB)
+        at[0] = ""
+        fail, fw = S("LST", 32, 48), S("LST", 64, 80)
+        vts(S("LST", 48, 64), S("wl", 1, 17), -1.0, float(NONE), ALU.mult, ALU.add, tag="wb")
+        vtt(fw, S("LST", 48, 64), fail, ALU.mult, tag="fw")
+        p = reg()
+        bcast(p, fail, 256, "bf")
+        act(S("FR", 0, 256), S(p, 0, 256), ACT.Copy, 0.0, 2.0)
+        firsts("LST", "OR", "I12", "EQo", "ooff", [S(ZO, h * ZW + LH, h * ZW + ZW) for h in range(H)])
+        for h in range(H):
+            vtt(S("tA", h * LH, h * LH + LH), (MTw, S("wu", h * NB, h * NB + NB)), row("OR", h), ALU.not_equal, tag="neM")
+            vtt(S("tA", 256 + h * LH, 256 + h * LH + LH), (NTw, S("ou", h * NB, h * NB + NB)), row("WR", h),
+                ALU.not_equal, tag="neN")
+        p = reg()
+        mm([(S(p, 0, 512), idn("I23"), S("tA", 0, 512)), (S(p, 0, 256), idn("I34"), S("FR", 0, 256)),
+            (S(p, 256, 512), idn("I34"), S("FR", 0, 256))], tag="B")
+        act(S("sB", 0, 512), S(p, 0, 512), ACT.Relu)
+        Pm = lambda a: S("Bm", 144 * a + 15 - (a + t) % 16, 144 * a + 143 - (a + t) % 16)
+        p = reg()
+        mm([(S(p, 0, 256), idn("nId"), S("sB", 0, 256))]
+           + [(S(p, h * LH, h * LH + LH), idn("nIf"), ep("EP", h)) for h in range(H)], tag="pM")
+        act(S("rM", 0, 256), S(p, 0, 256), ACT.Relu, 4096.0 * NONE)
+        p = reg()
+        mm([(S(p, 0, 256), idn("nId"), S("sB", 256, 512))]
+           + [(S(p, h * LH, h * LH + LH), idn("nIf"), ep("NP", h)) for h in range(H)]
+           + [(S(p, a, 256, 16), Pm(a), fail) for a in range(16)], tag="pN")
+        act(S("rN", 0, 256), S(p, 0, 256), ACT.Relu, float(NONE))
+        p = reg()
+        if last:
+            act(S("Mo", 0, 256), (MTw, S("ou", 0, 16)), ACT.Copy, 0.0, 4096.0)
+        mm([(S(p, 0, 256), idn("If"), S("Mo", 0, 256))] * last + [(S(p, a, 256, 16), Pm(a), fw) for a in range(16)],
+           each=not last, tag="pQ")
+        act(S("Q", 0, 256), S(p, 0, 256), ACT.Identity, float(NONE), 1.0 / 4096)
+        for b in range(14, -1, -2):
+            vtt((S("MC" if last else "NT", 0, WP), S("ooff", b, b + 2)), S("Q", 16 * b, 16 * b + 32),
+                S("rN", 16 * b, 16 * b + 32), ALU.subtract, tag="scN")
+        if last:
+            p = reg()
+            mm([(S(p, 0, 256), idn("If"), S("rM", 0, 256))]
+               + [(S(p, h * LH, h * LH + LH), idn("If"), ep("EP", h)) for h in range(H)], tag="pD")
+            act(S("dM", 0, 256), S(p, 0, 256), ACT.Identity, -4096.0 * NONE)
+            act(S("Yw", 0, 256), (S("MC", 0, W), S("wu", 0, 16)), ACT.Copy)
+        else:
+            p = reg()
+            for h in range(H):
+                zo, zb = S(ZO, h * ZW, h * ZW + LH), S(ZB, h * ZW, h * ZW + LH)
+                for u in range(2):
+                    o = S(p, 256 * u + h * LH, 256 * u + h * LH + LH)
+                    mm([(o, idn("Id"), zo), (o, idn("nId"), zb),
+                        (o, idn("nId" if u else "Id"), S("FR", h * LH, h * LH + LH))], tag="X1")
+            act(S("rX", 0, 512), S(p, 0, 512), ACT.Relu)
+            p = reg()
+            mm([(S(p, 0, 256), idn("Id"), S("rX", 0, 256)), (S(p, 0, 256), idn("nId"), S("rX", 256, 512)),
+                (S(p, 0, 256), idn("nId"), S("FR", 0, 256))]
+               + [(S(p, h * LH, h * LH + LH), idn("nId"), S(ZO, h * ZW, h * ZW + LH)) for h in range(H)], tag="X2")
+            act(S("x2", 0, 256), S(p, 0, 256), ACT.Identity, 31.0)
+            for b in range(14, -1, -2):
+                vcopy((S("XT", 0, WP), S("ooff", b, b + 2)), S("x2", 16 * b, 16 * b + 32), tag="scX")
+            p = S(reg(), 0, 16)
+            mm([(p, idn("ones"), fail)], tag="pS")
+            add("V", 64 * CYC, [p], [col(13)],
+                lambda q, R, p=p: q.tensor_reduce(R(col(13)), R(p), AxisListType.X, ALU.add, negate=True), tag="s")
+            vcopy(ci(13), col(13), tag="s")
+            vts(ci(14), ci(13), 31, None, AND, tag="s")
+            vts(col(12), ci(14), col(11), 32768.0, ALU.add, ALU.mult, tag="s")
+        for b in range(14, -1, -2):
+            u = (16 * b, 16 * b + 32)
+            vtt((S("MC" if last else "MT", 0, WP), S("woff", b, b + 2)), S("Yw", *u) if last else S("cN", 0, 32),
+                S("dM" if last else "rM", *u), ALU.subtract, tag="scM")
+    dma("Y", S("ynm", 0, 0), S("MC", 0, W), 3500)
+    dma("Y", S("yz", 0, 0), S("ZF", 0, 256), 300)
+    dma("Y", S("yw", 0, 0), S("WF", 0, 16), 100)
+    return ops
+
+
+def find_deps(ops):
+    hist = {}
+    for i, o in enumerate(ops):
+        d = {i - 1} if 0 < i < 8 else set()
+        acc = [(s, False) for s in o["rd"]] + [(s, True) for s in o["wr"]] + ([(o["dst"], True)] if "dst" in o else [])
+        acc = [(s[0], s[0][0] == "@", w) + ((0, 1 << 20) if s[0][0] == "@" or s[2] == 0 else (s[1], s[2])) for s, w in acc]
+        for name, psum, w, lo, hi in acc:
+            for j, a, b, pw in hist.get(name, []):
+                if j != i and b > lo and hi > a and (pw or w or (psum and ops[j]["eng"] != o["eng"])):
+                    d.add(j)
+        for name, psum, w, lo, hi in acc:
+            l = hist.setdefault(name, [])
+            if w and not psum:
+                l[:] = [e for e in l if e[0] == i or not (lo <= e[1] and e[2] <= hi)]
+            l.append((i, lo, hi, w))
+        o["deps"] = sorted(d)
+        o["wait"] = [j for j in o["deps"] if i >= 8 and (ops[j]["eng"] != "P" or o["eng"] != "P")]
+        o["regs"] = sorted(set(s[0] for s in o["rd"] + o["wr"] if s[0][0] == "@"))
+        o["succ"] = []
+        for j in o["deps"]:
+            ops[j]["succ"].append(i)
+
+
+def costs(ops, gath, scat, pcyc):
+    return [o["fix"] * pcyc if o["eng"] == "P" else o["fix"] + CYC * (gath * o["ge"] + scat * o["se"]) for o in ops]
+
+
+def pick(ready, free, rt, prio, look, later):
+    best = None
+    for e in "VSPGY":
+        cand = [(max(rt[i], free[e], later(i)), i) for i in ready[e]]
+        if cand:
+            t0 = min(cand)[0] + look
+            c = max([c for c in cand if c[0] <= t0], key=lambda c: (prio[c[1]], -c[1]))
+            if best is None or c[0] < best[0]:
+                best = c
+    return best
+
+
+def schedule(ops, cost, prio, look, hop):
+    n = len(ops)
+    users = {}
+    for o in ops:
+        for r in o["regs"]:
+            users[r] = users.get(r, 0) + 1
+    left = [len(o["deps"]) for o in ops]
+    ready = {e: [i for i in range(n) if left[i] == 0 and ops[i]["eng"] == e] for e in "VSPGY"}
+    free = {e: 0.0 for e in "VSPGY"}
+    fin, rt = [0.0] * n, [0.0] * n
+    bank, lastuse, held, rel, order, extra = {}, [[] for _ in range(8)], [False] * 8, [0.0] * 8, [], {}
+    while len(order) < n:
+        fb = min([(rel[b], b) for b in range(8) if not held[b]] + [(1e18, -1)])
+        st, i = pick(ready, free, rt, prio, look, lambda i: fb[0] if ops[i]["regs"] and ops[i]["regs"][0] not in bank else 0.0)
+        if st >= 1e17:
+            return None
+        o = ops[i]
+        if o["regs"] and o["regs"][0] not in bank:
+            bank[o["regs"][0]] = fb[1]
+            extra[i], lastuse[fb[1]] = [j for j in lastuse[fb[1]] if ops[j]["eng"] != "P"], []
+        free[o["eng"]] = st + cost[i]
+        fin[i] = st + cost[i] + o["lat"]
+        for r in o["regs"]:
+            users[r] -= 1
+            lastuse[bank[r]].append(i)
+            rel[bank[r]] = max(rel[bank[r]], fin[i] + hop)
+            held[bank[r]] = users[r] > 0
+        order.append(i)
+        ready[o["eng"]].remove(i)
+        for k in o["succ"]:
+            left[k] -= 1
+            if left[k] == 0:
+                rt[k] = max([fin[j] + hop for j in ops[k]["wait"]] + [0.0])
+                ready[ops[k]["eng"]].append(k)
+    return order, bank, extra, fin
+
+
+def backward(ops, cost, prio, look, hop):
+    n = len(ops)
+    left = [len(o["succ"]) for o in ops]
+    ready = {e: [i for i in range(n) if left[i] == 0 and ops[i]["eng"] == e] for e in "VSPGY"}
+    free = {e: 0.0 for e in "VSPGY"}
+    rt, end = [o["lat"] for o in ops], [0.0] * n
+    for _ in range(n):
+        st, i = pick(ready, free, rt, prio, look, lambda i: 0.0)
+        o = ops[i]
+        end[i] = free[o["eng"]] = st + cost[i]
+        ready[o["eng"]].remove(i)
+        for j in o["deps"]:
+            left[j] -= 1
+            rt[j] = max(rt[j], end[i] + (hop + ops[j]["lat"] if j in o["wait"] else 0))
+            if left[j] == 0:
+                ready[ops[j]["eng"]].append(j)
+    return end
+
+
+def replay(ops, plan, cost, hop):
+    free, fin = {}, {}
+    for i in plan[0]:
+        o = ops[i]
+        st = max([free.get(o["eng"], 0.0)] + [fin[j] + hop for j in o["wait"] + plan[2].get(i, [])])
+        free[o["eng"]] = st + cost[i]
+        fin[i] = st + cost[i] + o["lat"]
+    return max(fin.values())
+
+
+def best_plan(ops, tries):
+    cs = [costs(ops, *s[:3]) for s in SPEEDS]
+    c, hop, seed = cs[0], SPEEDS[0][3], [1]
+
+    def rnd(k):
+        seed[0] = (seed[0] * 1103515245 + 12345) % (1 << 31)
+        return (seed[0] >> 8) % k
+
+    def value(p):
+        return sum(w * replay(ops, p, x, s[3]) for w, x, s in zip((2.0, 1.1, 0.85, 0.8), cs, SPEEDS))
+    prio = [0.0] * len(ops)
+    for i in range(len(ops) - 1, -1, -1):
+        prio[i] = c[i] + ops[i]["lat"] + hop + max([prio[k] for k in ops[i]["succ"]] + [0.0])
+    early = "bf FR B sB pM pN rM rN neM neN Q pQ X1 X2 rX x2 dEQo EQo rEQo ooff fw".split()
+    best = schedule(ops, c, [p + 3000 * (o["tag"][-2:] == ".0" or o["tag"] in early) for p, o in zip(prio, ops)], 0, hop)
+    bv, tags = value(best), sorted(set(o["tag"] for o in ops))
+    for it in range(tries):
+        look = (0, 0, 20, 50)[rnd(4)]
+        if rnd(3) == 0:
+            e = backward(ops, c, [x + rnd(300) - 150 for x in best[3]], look, hop)
+        else:
+            e = [y + o["lat"] - x for x, y, o in zip(best[3], c, ops)]
+        t = rnd(5)
+        b = {tags[rnd(len(tags))]: (-3000, -1000, -500, -200, 200, 500, 1000, 3000)[rnd(8)] for _ in range((1, 2, 4)[rnd(3)])}
+        if rnd(2):
+            e = [x + (b.get(o["tag"], 0) if t > 2 or o["t"] == t else 0) for x, o in zip(e, ops)]
+        if rnd(2):
+            i, way, far, d = rnd(len(ops)), ("deps", "succ")[rnd(2)], (1500, 3000, 6000)[rnd(3)], (300, 1000, 2500)[rnd(3)]
+            cone, todo = {i}, [i]
+            while todo:
+                for j in ops[todo.pop()][way]:
+                    if j not in cone and abs(best[3][j] - best[3][i]) < far:
+                        cone.add(j)
+                        todo.append(j)
+            for j in cone:
+                e[j] += d if way == "deps" else -d
+        p = schedule(ops, c, e, look, hop)
+        if p:
+            v = value(p)
+            if v < bv + 1500.0 * max(0.0, 1 - it / (0.8 * tries)) * (rnd(1000) / 1000.0) ** 3:
+                best, bv = p, v
+    return best
+
+
+OPS = build_ops()
+find_deps(OPS)
+PLAN = best_plan(OPS, TRIES)
+SEMAPHORES = ["cV", "cS", "cP", "cG", "sent"] + ["d%d" % _i for _i, _o in enumerate(OPS) if _o["kind"] != "c"]
+
+
+def bits(m):
+    return bin(m).count("1")
+
+
+def rank_program(g, core, T, topo):
+    rank = T.rank_of(core)
+    if rank is None:
+        return
+    Q = {"V": g.vector, "S": g.scalar, "P": g.tensor, "G": g, "Y": g.sync}
+    order, bank, extra = PLAN[:3]
+
+    def R(s):
+        t = T["ps%d" % bank[s[0]]] if s[0][0] == "@" else T[s[0]]
+        if s[2] == 0:
+            return t[:]
+        return t[:, s[1]:s[2]] if s[3] == 1 else t[:, s[1]:s[2]:s[3]]
+
+    cnt = {e: 0 for e in "VSPG"}
+    known = {e: {} for e in "VSPGY"}
+    mark, clock, place, sent = {}, {}, {i: k for k, i in enumerate(order)}, 0
+    for i in order:
+        o = OPS[i]
+        e = o["eng"]
+        kn = known[e]
+        for j in sorted(o["wait"] + extra.get(i, []), key=lambda j: -place[j]):
+            sem, val = mark[j]
+            if kn.get(sem, 0) < val:
+                Q[e].wait_ge(T.sem[sem], val)
+                kn[sem] = val
+                for k, v in clock[j].items():
+                    kn[k] = max(kn.get(k, 0), v)
+        clock[i] = dict(kn)
+        if o["kind"] == "c":
+            cnt[e] += 1
+            o["fn"](Q[e], R).then_inc(T.sem["c" + e], 1)
+            mark[i] = ("c" + e, cnt[e])
+        elif o["kind"] == "d":
+            o["fn"](Q[e], R).then_inc(T.sem["d%d" % i], 16)
+            mark[i] = ("d%d" % i, 16)
+        else:
+            step = 1 + o["t"] % (NR - 1)
+            to, frm = T.cores[(rank + step) % NR], T.cores[(rank - step) % NR]
+            rid, pid = topo.addr(to)[:2]
+            m = topo.mask(core, to)
+            g.remote_dma(R(o["dst"]), R(o["src"]), T.sem["d%d" % i], T.sem.sent, pid, rid, m)
+            sent += bits(m)
+            mark[i] = ("d%d" % i, bits(topo.mask(frm, core)))
+            clock[i] = {}
+    for e in "VSPG":
+        g.wait_ge(T.sem["c" + e], cnt[e])
+    g.wait_ge(T.sem.sent, sent)
+    for i, o in enumerate(OPS):
+        if o["kind"] != "c":
+            g.wait_ge(T.sem[mark[i][0]], mark[i][1])

@@ -5,39 +5,48 @@ ACT = ActivationFunctionType
 RO, NR, W, NONE = 3, 8, 2048, 2047
 H = 2
 REP = 4
+KS = (2, 2, 4, 4, 4)
+GREP = True
+TWO = False
+MS = 1
 XV = ((), (3,))
-TRIES = 1500
+XS = 2
+TRIES, MOVES, HEAT = 1200, 40000, 300.0
+WEIGHTS, LATS = (2.0, 0.0, 0.85, 0.8), (1.0, 1.0, 1.3, 1.3)
 SPEEDS = [(1.5, 3.8, 0.42, 110.0), (1.1, 2.0, 0.42, 110.0), (2.0, 5.5, 0.42, 160.0), (1.5, 3.8, 0.6, 200.0)]
 NB = 16 // H
 LH = 16 * NB
 EW = LH + 32
 TW = 2 * LH + 32
-ZW = LH + NB
 WP = W + 32
+NL = 9
+ZP, XN, RB = 35.0, 48.0, 384
 F32, BF, F16, I32, U16 = "float32", "bfloat16", "float16", "int32", "uint16"
 
 SCRATCH = {_n: ("sbuf", [128, _c], _d) for _n, _c, _d in [
-    ("nmi", W, I32), ("NI", W, I32), ("NT", WP, F32), ("MT", WP, F32), ("MC", WP, F32), ("XT", WP, BF),
-    ("zin", 256, BF), ("thi", 4, I32), ("col", 32, F32), ("coli", 32, I32),
-    ("ones", 2304, BF), ("m4", 2304, BF), ("Sel", 2048, BF), ("Bm", 2304, BF), ("Bt", 2304, BF), ("Bu", 2304, BF),
-    ("B1", 144, BF), ("B15", 144, BF), ("B0", 144, BF), ("Bn", 144, BF),
-    ("Id", 128, BF), ("nId", 128, BF), ("I12", 128, BF), ("I23", 128, BF), ("I24", 128, BF), ("I34", 128, BF),
-    ("If", 128, F32), ("nIf", 128, F32), ("KC", 256, BF), ("iC", 16, F32), ("pm", 16, U16), ("cN", 32, F32),
-    ("wu", 16, U16), ("ou", 16, U16), ("wl", 32, F16), ("LST", 80, F16), ("thr", 16, F32),
+    ("nmi", W, I32), ("NI", W, I32), ("NT", WP, F32), ("MT", WP, F32), ("ME", WP, F32), ("MC", WP, F32), ("XT", WP, BF),
+    ("thi", 4, I32), ("col", 32, F32), ("coli", 32, I32),
+    ("ones", 576, BF), ("Sel", 2048, BF), ("Bm", 2304, BF), ("Bt", 2304, BF),
+    ("B1", 144, BF), ("B15", 144, BF), ("B0", 144, BF),
+    ("Id", 128, BF), ("nId", 128, BF), ("I12", 128, BF), ("nI12", 128, BF), ("I11", 128, BF), ("nI11", 128, BF),
+    ("IR", 128, BF), ("Im10", 128, BF), ("I15", 128, BF), ("nI27", 128, BF), ("I28", 128, BF),
+    ("I27", 128, BF), ("nI28", 128, BF),
+    ("Ie", 256, BF), ("Ie12", 256, BF), ("If", 128, F32), ("rp", 2, U16), ("o4", 32 * H, F16), ("E0", 256, I32),
+    ("H47", 128, F16), ("Hn", 128, F16), ("KF", LH, F32), ("KC", 2 * LH, F16), ("cN", 32, F32),
+    ("wu", 16, U16), ("ou", 16, U16), ("LST", 112, F16),
     ("KEY", 16, I32), ("oi", 16, I32), ("KEY2", 16, I32), ("wand", 16, I32),
-    ("EP", H * EW, F32), ("NP", H * EW, F32), ("TE", H * TW, F32), ("TN", H * TW, F32),
-    ("eoff", 256, U16), ("uoff", 256, U16), ("ETf", 256, F32), ("UTf", 256, F32),
-    ("WR", REP * 256, F32), ("OR", REP * 256, F32), ("FR", 256, BF),
-    ("EQN", 4096, BF), ("XG", 4096, BF), ("AD", 4096, BF), ("EQM", 4096, BF), ("CN", 4096, BF),
-    ("SG", 256, BF), ("SG2", 256, BF), ("RUN", 64 * H, F32), ("RUN2", 64 * H, F32), ("FB", 64 * H, F32),
+    ("EP", H * EW, F16), ("NP", H * EW, F16), ("TE", H * TW, F16), ("TN", H * TW, F16),
+    ("eoff", 256, U16), ("uoff", 256, U16), ("ETf", 256, F16), ("UTf", 256, F16),
+    ("WR", REP * 256, F32), ("OR", 256, F32), ("FR", 256, BF),
+    ("EQN", 4096, BF), ("XG", 4096, BF), ("AD", 4096, BF), ("EQM", 4096, BF), ("MG", 4096, F16),
+    ("SG", 256, BF), ("SG2", 256, BF), ("CT", 256, BF), ("RUN", 64 * H, F32), ("RUN2", 64 * H, F32),
     ("TR", 64 * H, F32), ("TR2", 64 * H, F32),
-    ("EQw", 512, BF), ("EQo", 512, BF), ("woff", 16, U16), ("ooff", 16, U16),
-    ("tA", 512, BF), ("sB", 512, BF), ("rM", 256, F32), ("rN", 256, F32), ("Q", 256, F32),
-    ("Mo", 256, F32), ("dM", 256, F32), ("Yw", 256, F32), ("rX", 512, BF), ("x2", 256, BF),
-    ("WI0", 16, I32), ("WI1", 16, I32), ("WI2", 16, I32), ("WF", 16, F32),
+    ("EQ", 1024, BF), ("off", 32, U16), ("NE", 512, F16), ("rM", 256, F32), ("nA", 256, F32), ("nB", 256, F32),
+    ("Mo", 256, F32), ("Yw", 256, F32), ("x1", 256, BF), ("x2", 256, BF),
+    ("WI0", 64 * H, I32), ("WI1", 64 * H, I32), ("WI2", 64 * H, I32), ("WF", 16, F32),
     ("WO0", 16, I32), ("WO1", 16, I32), ("WOF", 16, F32),
-    ("ZB0", H * ZW, BF), ("ZB1", H * ZW, BF), ("ZB2", H * ZW, BF), ("ZF", 256, BF),
-    ("ZO0", H * ZW, BF), ("ZO1", H * ZW, BF), ("ZO2", H * ZW, BF)]}
+    ("ZB0", 256, BF), ("ZB1", 256, BF), ("ZB2", 256, BF), ("ZF", 256, BF),
+    ("ZO0", 256, BF), ("ZO1", 256, BF), ("ZO2", 256, BF)]}
 for _i in range(8):
     SCRATCH["ps%d" % _i] = ("psum", [128, 512], F32)
 
@@ -104,26 +113,27 @@ def build_ops():
         add("V", max(64, _n(out) * (0.5 if _two(out) else 1)) * CYC, [], [out], lambda q, R: q.memset(R(out), c))
 
     def vtr(out, in_):
-        vec(out, [in_], 1, lambda q, R: q.transpose(R(out), R(in_)), "")
+        vec(out, [in_], 0.5 if _two(out, in_) else 1, lambda q, R: q.transpose(R(out), R(in_)), "")
 
     def act(out, in_, f, bias=0.0, scale=1.0, tag=""):
         ind = len(in_) == 2
         add("S", 65 + (0 if ind else CYC * _n(out)), flat(in_, bias, scale), [out],
             lambda q, R: q.activation(R(out), opnd(R, in_), f, opnd(R, bias), opnd(R, scale)), tag=tag, ge=_n(out) if ind else 0)
 
-    def mm(lst, start=True, stop=True, each=False, tag=""):
+    def mm(lst, start=True, stop=True, each=0, tag=""):
         c = sum(max(64, _n(r)) * (4 if SCRATCH[r[0]][2] == F32 else 1) for o, l, r in lst)
 
         def fn(q, R):
             ins = None
             for i, (o, l, r) in enumerate(lst):
-                ins = q.matmul(R(o), R(l), R(r), each or (start and i == 0), each or (stop and i == len(lst) - 1))
+                a, b = (i % each == 0, i % each == each - 1) if each else (start and i == 0, stop and i == len(lst) - 1)
+                ins = q.matmul(R(o), R(l), R(r), a, b)
             return ins
         add("P", c + 64, [x[1] for x in lst] + [x[2] for x in lst], [x[0] for x in lst], fn, tag=tag)
 
-    def gsel(out, in_, pat, op, base, cm):
+    def gsel(out, in_, pat, op, base, cm, tag=""):
         add("G", 170 + 2 * CYC * _n(out), [in_], [out],
-            lambda q, R: q.affine_select(R(out), R(in_), pat, op, 0.0, base, cm))
+            lambda q, R: q.affine_select(R(out), R(in_), pat, op, 0.0, base, cm), tag=tag)
 
     def giota(out, pat, base, cm):
         kw = {} if SCRATCH[out[0]][2] == I32 else {"allow_small_or_imprecise_dtypes": True}
@@ -140,88 +150,119 @@ def build_ops():
     ci = lambda j: S("coli", j, j + 1)
     idn = lambda n, a=0: S(n, 128 * a, 128 * a + 128)
     Bw = lambda n, a: S(n, 15 - a, 143 - a)
+    lst = lambda j, n=1: S("LST", 16 * j, 16 * (j + n))
     NTw, MTw, XTw = S("NT", 0, W), S("MT", 0, W), S("XT", 0, W)
-    BIG = 1.5 * 2.0 ** 35
+    BIG, TOP = 1.5 * 2.0 ** 35, 4096.0 * NONE
+    FAR = TOP + 2.0 ** 29
     AND, SHR = ALU.bitwise_and, ALU.arith_shift_right
 
-    dma("Y", S("WI0", 0, 16), S("w", 0, 0), 100)
+    for h in range(H):
+        dma("Y", S("WI0", 64 * h, 64 * h + NB), S("w", h * NB, h * NB + NB), 100)
     for c in range(4):
         dma("Y", S("nmi", 512 * c, 512 * c + 512), S("nm", 512 * c, 512 * c + 512), 870 * (c + 1))
-    dma("Y", S("zin", 0, 256), S("z", 0, 0), 3600)
+    dma("Y", S("ZB0", 0, 256), S("z", 0, 0), 3600)
     dma("Y", XTw, S("x", 0, 0), 5200)
     dma("Y", S("thi", 0, 1), S("th", 0, 0), 5200)
     giota(ci(0), [[0, 1]], 0, 1)
-    vset(S("ones", 0, 2304), 1.0)
+    vset(S("ones", 0, 576), 1.0)
     gsel(idn("Id"), idn("ones"), [[-1, 128]], ALU.is_equal, 0, 1)
-    gsel(S("Sel", 0, 2048), S("ones", 0, 2048), [[-1, 16], [-16, 8], [0, 16]], ALU.is_equal, 0, 1)
-    giota(S("iC", 0, NB), [[16 // NB, NB]], 0, 0)
+    for a in range(0, 16, 4):
+        gsel(S("Sel", 128 * a, 128 * a + 512), S("ones", 0, 512), [[-1, 4], [-16, 8], [0, 16]], ALU.is_equal, -a, 1)
     gsel(S("B0", 0, 144), S("ones", 0, 144), [[-16, 9], [256, 16]], ALU.is_ge, -256 * 15, 1)
     gsel(S("B1", 0, 144), S("B0", 0, 144), [[16, 9], [0, 16]], ALU.is_ge, 15, -1)
-    giota(S("KC", 0, LH), [[2048, 16], [0, NB]], 0, 0)
-    act(S("m4", 0, 2304), S("ones", 0, 2304), ACT.Copy, 0.0, -4096.0)
-    gsel(S("Bm", 0, 2304), S("m4", 0, 2304), [[-1, 16], [-16, 9], [256, 16]], ALU.is_equal, -256 * 15, 1)
-    gsel(S("Bu", 0, 2304), S("m4", 0, 2304), [[0, 16], [-16, 9], [256, 16]], ALU.is_ge, -256 * 15, 1)
-    gsel(S("Bt", 0, 2304), S("Bu", 0, 2304), [[1, 16], [16, 9], [0, 16]], ALU.is_ge, -1, -1)
+    giota(S("KF", 0, LH), [[1, 16], [0, NB]], 0, 0)
+    for a in range(0, 16, 4):
+        gsel(S("Bm", 144 * a, 144 * a + 576), S("ones", 0, 576), [[-1, 4], [-16, 9], [256, 16]], ALU.is_equal, -256 * 15 - a, 1)
+    for a in range(16):
+        gsel(S("Bt", 144 * a, 144 * a + 144), S("B0", 0, 144), [[16, 9], [0, 16]], ALU.is_ge, a - 1, -1)
     act(S("B15", 0, 144), S("B1", 0, 144), ACT.Copy, 0.0, 32768.0)
-    act(S("Bn", 0, 144), S("B1", 0, 144), ACT.Copy, 0.0, -4096.0)
-    for n, v in (("nId", -1.0), ("I12", 4096.0), ("I23", 2.0 ** 23), ("I24", -2.0 ** 24), ("I34", -2.0 ** 34),
-                 ("If", 1.0), ("nIf", -1.0)):
+    for n, v in (("nId", -1.0), ("I12", 4096.0), ("nI12", -4096.0), ("I11", 2048.0), ("IR", -RB * 32768.0),
+                 ("Im10", 1.0 / 1024), ("I15", 32768.0), ("nI27", -2.0 ** 27), ("I28", 2.0 ** 28), ("If", 1.0),
+                 ("I27", 2.0 ** 27), ("nI28", -2.0 ** 28), ("H47", -float(NONE)), ("Hn", NONE / 2.0)):
         act(idn(n), idn("Id"), ACT.Copy, 0.0, v)
+    vts(S("KC", 0, LH), S("KF", 0, LH), (RB - 512) * 16.0, None, ALU.add)
+    vcopy(S("KC", LH, 2 * LH), S("KF", 0, LH))
     vts(ci(1), ci(0), 15, None, AND)
     vts(ci(2), ci(0), 4, 1, SHR, AND)
-    vts(ci(3), ci(0), NB - 2, None, AND)
-    vts(ci(4), ci(0), 1, None, AND)
-    vts(ci(5), ci(0), {16: 4, 8: 3}[NB], 16 // NB - 1, SHR, AND)
-    vcopy(S("col", 1, 6), S("coli", 1, 6))
-    vts(col(6), col(4), col(2), None, ALU.not_equal)
-    vts(col(7), col(2), -32.0, float(LH + 32), ALU.mult, ALU.add)
-    vts(col(8), col(3), col(2), 16.0, ALU.add, ALU.mult)
-    vts(col(9), col(6), col(7), col(5), ALU.mult, ALU.add)
-    vts(S("pm", 0, NB), S("iC", 0, NB), col(8), col(9), ALU.add, ALU.add)
-    vts(col(15), col(1), -1.0, -float(W), ALU.mult, ALU.add)
-    vts(col(16), col(1), -1.0, -float(W + 16), ALU.mult, ALU.add)
+    vts(ci(3), ci(0), NB - 1, None, AND)
+    vcopy(S("col", 1, 3), S("coli", 1, 3))
+    vts(col(3), col(2), -4.0, 4.0, ALU.mult, ALU.add)
+    vts(col(4), col(2), 4.0, None, ALU.mult)
+    for u in range(2):
+        act(idn("Ie", u), idn("Id"), ACT.Copy, 0.0, col(3 + u))
+        vts(col(15 + u), col(1), float(W + 16 * u), None, ALU.add)
+        vcopy(S("rp", u, u + 1), ci(3))
+    act(S("Ie12", 0, 256), S("Ie", 0, 256), ACT.Copy, 0.0, 1024.0)
     vset(S("EP", 0, H * EW), 0.0)
     vset(S("NP", 0, H * EW), 0.0)
-    vset(S("FB", 0, 64 * H), 2.0 ** 24)
-    vset(S("cN", 0, 32), 4096.0 * NONE)
-    vts(S("wl", 0, 1), col(1), 0.0, -1.0, ALU.mult, ALU.add)
-    vts(S("LST", 0, 1), col(1), 0.0, -1.0, ALU.mult, ALU.add)
+    for t in range(RO):
+        for h in range(H):
+            vset(S("WI%d" % t, 64 * h + NB, 64 * h + 64), 2 ** 24)
+    vset(S("cN", 0, 32), FAR)
     vts(col(11), S("thi", 0, 1), -512.0, None, ALU.add)
     vts(col(12), col(11), 32768.0, None, ALU.mult)
     for c in range(4):
         a, b = 512 * c, 512 * c + 512
-        vts(S("NI", a, b), S("nmi", a, b), 4095, None, AND)
         vts(S("MT", a, b), S("nmi", a, b), BIG, -BIG, ALU.add, ALU.add)
-        vcopy(S("NT", a, b), S("NI", a, b))
-    vset(S("MT", NONE, W), 4096.0 * W)
-    vset(S("XT", NONE, W), 40.0)
-    for h in range(H):
-        act(S("ZB0", h * ZW, h * ZW + LH), S("zin", h * LH, h * LH + LH), ACT.Identity, 31.0, -1.0)
-        vset(S("ZB0", h * ZW + LH, h * ZW + ZW), 0.0)
+        vts(S("NI", a, b), S("nmi", a, b), 4095, None, AND)
+        act(S("MC", a, b), S("MT", a, b), ACT.Relu, -2.0 ** 29 * (NONE - 1), 2.0 ** 17)
+        act(S("NT", a, b), S("NI", a, b), ACT.Copy)
+        if c % 2:
+            dma("G", S("MT", a - 512, b), S("MC", a - 512, b), 2500, acc=True)
+    vset(S("XT", NONE, W), XN)
+    if TWO:
+        dma("Y", S("ME", 0, W), MTw, 3500)
 
     ep = lambda n, h: S(n, h * EW + 16, h * EW + 16 + LH)
-    row = lambda n, h, r=0: S(n, (h * REP + r) * LH, (h * REP + r + 1) * LH)
+    row = lambda n, h, r=0, m=1: S(n, (h * REP + r) * LH, (h * REP + r + m) * LH)
 
-    def bcast(ps, src, width, tag):
-        mm([(S(ps, a, width, 16), idn("Sel", a), src) for a in range(16)], each=True, tag=tag)
+    def bcast(ps, src, tag):
+        mm([(S(ps, a, 16 * _n(src), 16), idn("Sel", a), src) for a in range(16)], each=1, tag=tag)
 
-    def turn(h, pad, tr, off, tf, scale):
-        e0, t0 = h * EW, h * TW
+    def rows(name, h, src, tag):
+        p = reg()
+        bcast(p, src, tag)
+        for r in range(1 if GREP else REP):
+            act(row(name, h, r), S(p, 0, LH), ACT.Copy, 0.0, 4096.0)
+        r = 1
+        while GREP and r < REP:
+            gsel(row(name, h, r, r), row(name, h, 0, r), [[0, r * LH]], ALU.is_ge, 0, 0)
+            r *= 2
+
+    def turn(h, pad, tr, off, tf, mask):
+        e0, t0, p = h * EW, h * TW, reg()
         vtr(S(tr, t0, t0 + LH), ep(pad, h))
         vtr(S(tr, t0 + LH, t0 + TW), S(pad, e0, e0 + EW))
-        win = (S(tr, t0, t0 + TW), S("pm", 0, NB))
-        vts(S(off, h * LH, h * LH + LH), win, scale, None, ALU.mult)
-        act(S(tf, h * LH, h * LH + LH), win, ACT.Copy, 0.0, scale)
+        src = lambda b, u: t0 + 16 * u + (32 * (b // 2) if b % 2 == u else LH + 32 * ((b + 1) // 2))
+        mm([(S(p, b, LH, NB), idn(mask, u), S(tr, src(b, u), src(b, u) + 16)) for b in range(NB) for u in range(2)],
+           each=2, tag="t" + off)
+        vts(S(off, h * LH, h * LH + LH), S(p, 0, LH), float(NONE), None, ALU.min)
+        vcopy(S(tf, h * LH, h * LH + LH), S(off, h * LH, h * LH + LH))
 
-    def keys(h, eq, val, sg, tf, run, tr, first, key):
+    def compare(h, out, win, off, rw):
+        k = 0
+        for n in KS:
+            d = (16 * h + k) * LH
+            vtt(S(out, d, d + n * LH), (win, S(off, h * LH + k * NB, h * LH + (k + n) * NB)), row(rw, h, 0, n),
+                ALU.is_equal, tag=out + str(k * NB // 64))
+            k += n
+
+    def keys(h, eq, val, sg, tf, kc, run, tr, first, key):
         for c in range(LH // 64):
             d0, k0, u = h * 16 * LH + 1024 * c, h * LH + 64 * c, val + str(c)
             pc, pk = S(reg(), 0, 64), S(reg(), 0, 64)
             mm([(pc, Bw("B1", a), S(eq, d0 + a, d0 + 1024, 16)) for a in range(16)], tag="C" + u)
             act(S(sg, k0, k0 + 64), pc, ACT.Sign)
-            mm([(pk, idn("Id"), S("KC", 64 * c, 64 * c + 64)), (pk, idn("If"), S(tf, k0, k0 + 64))]
-               + [(pk, Bw("B15", a), S(val, d0 + a, d0 + 1024, 16)) for a in range(16)], stop=False, tag="K" + u)
-            mm([(pk, idn("I24"), S(sg, k0, k0 + 64))], start=False, tag="L" + val)
+            low = [(pk, idn("I11"), S("KC", kc + 64 * c, kc + 64 * c + 64)), (pk, idn("Id"), S(tf, k0, k0 + 64))]
+            flag = [(pk, idn("IR"), S(sg, k0, k0 + 64))]
+            if first is None:
+                mm(low + [(pk, Bw("B15", a), S(val, d0 + a, d0 + 1024, 16)) for a in range(16)], stop=False, tag="K" + u)
+                mm(flag, start=False, tag="L" + val)
+            else:
+                pn = S(reg(), 0, 64)
+                mm([(pn, Bw("B1", a), S(val, d0 + a, d0 + 1024, 16)) for a in range(16)], tag="K" + u)
+                act(S("CT", k0, k0 + 64), pn, ACT.Identity, 192.0, -1.0 / 32768)
+                mm(low + [(pk, idn("I15"), S("CT", k0, k0 + 64))] + flag, tag="L" + val)
             r = S(run, 64 * h, 64 * h + 64)
             if c == 0 and first is None:
                 vts(r, pk, 2.0 ** 24 - 1, None, ALU.min)
@@ -232,169 +273,159 @@ def build_ops():
             vtt(key if n == NB else S(tr, to, to + n), S(src, a, a + n), S(src, a + n, a + 2 * n), ALU.min, tag=run)
             src, a, to, n = tr, to, to + n, n // 2
 
-    def firsts(lst, rw, scale, eq, off, more):
-        pd, pr = reg(), S(reg(), 0, 16)
-        mm([(S(pd, a, 272, 16), idn(scale), S(lst, 0, 17)) for a in range(16)], each=True, tag="d" + eq)
-        for h in range(H):
-            for d in range(2):
-                vtt(S(eq, 256 * d + h * LH, 256 * d + h * LH + LH), S(pd, 16 - 16 * d + h * LH, 16 - 16 * d + h * LH + LH),
-                    row(rw, h), ALU.is_equal)
-        mm([(pr, idn("nId"), S(lst, 1, 17))] + [(S(pr[0], h * NB, h * NB + NB), idn("nId"), x) for h, x in enumerate(more)]
-           + [(pr, S("Bt", 143 * a + 15, 143 * a + 143), S(eq, a, 256, 16)) for a in range(16)]
-           + [(pr, Bw("Bn", a), S(eq, 256 + a, 512, 16)) for a in range(16)], tag="r" + eq)
-        for u in range(2):
-            vts(S(off, u, 16, 2), S(pr[0], u, 16, 2), col(15 + u), -1.0, ALU.max, ALU.mult)
+    def scatter(table, o0, a, b, op, tag):
+        for k in range(14, -1, -2):
+            u = lambda s: S(s, 16 * k, 16 * k + 32) if SCRATCH[s][1][1] > 32 else S(s, 0, 32)
+            out = (S(table, 0, WP), S("off", o0 + k, o0 + k + 2))
+            if b:
+                vtt(out, u(a), u(b), op, tag=tag)
+            else:
+                vcopy(out, u(a), tag=tag)
 
     for t in range(RO):
         last = t == RO - 1
         at[1] = t
         WI, ZB, ZO = "WI%d" % t, "ZB%d" % t, "ZO%d" % t
         if last:
-            dma("Y", S("MC", 0, W), NTw, 3500)
-            dma("G", S("MC", 0, W), MTw, 5000, acc=True)
-            vset(S("MC", NONE, W), 4097.0 * NONE)
+            for c in range(0, W, 512):
+                vts(S("MC", c, c + 512), S("MT", c, c + 512), TOP, None, ALU.min)
+            dma("G", S("MC", 0, W), NTw, 5000, acc=True)
         for h in range(H):
             at[0] = "." + str(h)
-            b0, b1, l0, d0, r0 = h * NB, h * NB + NB, h * LH, h * 16 * LH, h * REP * LH
-            zb = S(ZB, h * ZW, h * ZW + LH)
-            vcopy(S("wu", b0, b1), S(WI, b0, b1))
-            vcopy(S("wl", 1 + b0, 1 + b1), S(WI, b0, b1))
+            b0, b1, l0, d0 = h * NB, h * NB + NB, h * LH, h * 16 * LH
+            zb, wi = S(ZB, l0, l0 + LH), S(WI, 64 * h, 64 * h + NB)
+            vcopy(S("wu", b0, b1), wi)
+            vts(S("LST", 16 + b0, 16 + b1), wi, 1.0 / 4096, None, ALU.mult, tag="ws")
             if t:
-                vcopy(ep("EP", h), (MTw, S("wu", b0, b1)))
+                act(ep("EP", h), (S("ME", 0, W) if TWO else MTw, S("wu", b0, b1)), ACT.Copy, 0.0, 2.0 ** -14)
             else:
-                vts(ep("EP", h), (S("nmi", 0, W), S("wu", b0, b1)), BIG, -BIG, ALU.add, ALU.add)
-            turn(h, "EP", "TE", "eoff", "ETf", 1.0 / 4096)
-            p = reg()
-            bcast(p, S("wl", 1 + b0, 1 + b1), LH, "bw")
-            for r in range(REP):
-                act(row("WR", h, r), S(p, 0, LH), ACT.Copy)
-            act(S("thr", b0, b1), S(ZB, h * ZW + LH, h * ZW + ZW), ACT.Identity, col(12), -8192.0)
-            vts(S("FB", 64 * h, 64 * h + NB), S(WI, b0, b1), -2.0 ** 23, None, ALU.add)
-            for k in range(0, 16, REP):
-                vtt(S("EQN", d0 + k * LH, d0 + (k + REP) * LH),
-                    (NTw if t else S("NI", 0, W), S("eoff", l0 + k * NB, l0 + (k + REP) * NB)),
-                    S("WR", r0, r0 + REP * LH), ALU.is_equal, tag="EQN%d" % (k * NB // 64))
-            kp = 512 // LH
+                vts(S("E0", l0, l0 + LH), (S("nmi", 0, W), S("wu", b0, b1)), 12, None, SHR)
+                vts(ep("EP", h), S("E0", l0, l0 + LH), 0.25, None, ALU.mult)
+            turn(h, "EP", "TE", "eoff", "ETf", "Ie")
+            rows("WR", h, S("LST", 16 + b0, 16 + b1), "bw")
+            compare(h, "EQN", NTw if t else S("NI", 0, W), "eoff", "WR")
+            kp, c0 = 512 // LH, 0
             for c in range(16 // kp):
                 xg, ad = S("XG", d0 + 512 * c, d0 + 512 * c + 512), S("AD", d0 + 512 * c, d0 + 512 * c + 512)
                 if c in XV[h]:
                     for k in range(kp):
                         o0 = l0 + (c * kp + k) * NB
-                        vtt(S("XG", xg[1] + k * LH, xg[1] + k * LH + LH), (XTw, S("eoff", o0, o0 + NB)), zb, ALU.add, tag="xV")
-                    act(ad, xg, ACT.Abs, -31.0, tag="AD%d" % c)
-                else:
-                    act(xg, (XTw, S("eoff", l0 + 32 * c, l0 + 32 * c + 32)), ACT.Copy, tag="xS%d" % c)
-                    p = reg()
-                    mm([(S(p, 0, 512), idn("Id"), xg)] + [(S(p, k * LH, k * LH + LH), idn("Id"), zb) for k in range(kp)], tag="xP")
-                    act(ad, S(p, 0, 512), ACT.Abs, -31.0, tag="AD%d" % c)
-            keys(h, "EQN", "AD", "SG", "ETf", "RUN", "TR", None, S("KEY", b0, b1))
+                        vtt(S("XG", xg[1] + k * LH, xg[1] + k * LH + LH), (XTw, S("eoff", o0, o0 + NB)), zb, ALU.subtract, tag="xV")
+                    act(ad, xg, ACT.Abs, tag="AD%d" % c)
+                    continue
+                if c >= c0:
+                    c0 = c + 1
+                    while c0 < 16 // kp and c0 - c < XS and c0 not in XV[h]:
+                        c0 += 1
+                    act(S("XG", xg[1], d0 + 512 * c0), (XTw, S("eoff", l0 + 32 * c, l0 + 32 * c0)), ACT.Copy, tag="xS%d" % c)
+                p = reg()
+                mm([(S(p, 0, 512), idn("Id"), xg)] + [(S(p, k * LH, k * LH + LH), idn("nId"), zb) for k in range(kp)], tag="xP")
+                act(ad, S(p, 0, 512), ACT.Abs, tag="AD%d" % c)
+            keys(h, "EQN", "AD", "SG", "ETf", 0, "RUN", "TR", None, S("KEY", b0, b1))
             vts(S("oi", b0, b1), S("KEY", b0, b1), NONE, None, AND)
             vcopy(S("ou", b0, b1), S("oi", b0, b1))
-            vcopy(S("LST", 1 + b0, 1 + b1), S("oi", b0, b1), tag="ol")
-            vtt(S("LST", 32 + b0, 32 + b1), S("KEY", b0, b1), S("thr", b0, b1), ALU.is_ge, tag="fail")
-            vts(S(ZO, h * ZW + LH, h * ZW + ZW), S("oi", b0, b1), float(NONE), 4096.0, ALU.is_equal, ALU.mult, tag="FL")
+            vts(S("LST", b0, b1), S("oi", b0, b1), 0.25, None, ALU.mult, tag="ol")
+            act(S("o4", 32 * h, 32 * h + 32), (S("oi", b0, b1), S("rp", 0, 2)), ACT.Copy, 0.0, 0.25)
+            if t == 0:
+                act(ep("EP", h), (MTw, S("wu", b0, b1)), ACT.Copy, 0.0, 2.0 ** -14, tag="EQ")
         at[0] = ""
         if last:
             vset(S("XT", NONE, W), 255.0)
-        firsts("wl", "WR", "Id", "EQw", "woff", [])
         for h in range(H):
             at[0] = "." + str(h)
-            b0, b1, l0, d0, r0 = h * NB, h * NB + NB, h * LH, h * 16 * LH, h * REP * LH
-            zo = S(ZO, h * ZW, h * ZW + LH)
-            vcopy(ep("NP", h), (NTw, S("ou", b0, b1)))
-            turn(h, "NP", "TN", "uoff", "UTf", 1.0)
-            p = reg()
-            bcast(p, S("LST", 1 + b0, 1 + b1), LH, "bo")
-            for r in range(REP):
-                act(row("OR", h, r), S(p, 0, LH), ACT.Copy, 0.0, 4096.0)
+            b0, b1, l0, d0 = h * NB, h * NB + NB, h * LH, h * 16 * LH
+            zo = S(ZO, l0, l0 + LH)
+            act(ep("NP", h), (NTw, S("ou", b0, b1)), ACT.Copy, 0.0, 1.0 / 4096)
+            turn(h, "NP", "TN", "uoff", "UTf", "Ie12")
+            po = reg()
+            bcast(po, S("o4", 32 * h, 32 * h + 32), "bo")
+            act(S("OR", l0, l0 + LH), S(po, 0, LH), ACT.Copy, 0.0, 4096.0)
             if last:
                 act(zo, (XTw, S("ou", b0, b1)), ACT.Copy, tag="xo")
-                send(S("ZF", l0, l0 + LH), zo, 256 * LH)
             else:
-                act(zo, (XTw, S("ou", b0, b1)), ACT.Relu, 31.0, -1.0, tag="xo")
-                send(S("ZB%d" % (t + 1), h * ZW, h * ZW + ZW), S(ZO, h * ZW, h * ZW + ZW), 256 * ZW)
-            for k in range(0, 16, REP):
-                vtt(S("EQM", d0 + k * LH, d0 + (k + REP) * LH), (MTw, S("uoff", l0 + k * NB, l0 + (k + REP) * NB)),
-                    S("OR", r0, r0 + REP * LH), ALU.is_equal, tag="EQM%d" % (k * NB // 64))
-            for c in range(LH // 32):
-                act(S("CN", d0 + 512 * c, d0 + 512 * c + 512), (MTw, S("uoff", l0 + 32 * c, l0 + 32 * c + 32)),
-                    ACT.Sign, 4096.0 * NONE, -1.0, tag="CN%d" % (c // 2))
-            keys(h, "EQM", "CN", "SG2", "UTf", "RUN2", "TR2", S("FB", 64 * h, 64 * h + 64), S("KEY2", b0, b1))
+                vts(zo, (XTw, S("ou", b0, b1)), ZP, None, ALU.min, tag="xo")
+            send(S("ZF" if last else "ZB%d" % (t + 1), l0, l0 + LH), zo, 256 * LH)
+            for c in range(0, 4, MS):
+                act(S("MG", d0 + 512 * c, d0 + 512 * (c + MS)), (MTw, S("uoff", l0 + 32 * c, l0 + 32 * (c + MS))),
+                    ACT.Copy, 0.0, 2.0 ** -14, tag="MG%d" % (c // 2))
+            for c in range(4):
+                d = d0 + 512 * c
+                vtt(S("EQM", d, d + 512), S("MG", d, d + 512), S(po, 0, 512), ALU.is_equal, tag="EQM%d" % (c // 2))
+            keys(h, "EQM", "MG", "SG2", "UTf", LH, "RUN2", "TR2", S(WI, 64 * h, 64 * h + 64), S("KEY2", b0, b1))
             if last:
                 vts(S("wand", b0, b1), S("KEY2", b0, b1), NONE, None, AND)
                 vcopy(S("WOF", b0, b1), S("wand", b0, b1))
                 send(S("WF", b0, b1), S("WOF", b0, b1), 512 * NB)
             else:
                 vts(S("WO%d" % t, b0, b1), S("KEY2", b0, b1), NONE, None, AND, tag="wand")
-                send(S("WI%d" % (t + 1), b0, b1), S("WO%d" % t, b0, b1), 512 * NB)
+                send(S("WI%d" % (t + 1), 64 * h, 64 * h + NB), S("WO%d" % t, b0, b1), 512 * NB)
         at[0] = ""
-        fail, fw = S("LST", 32, 48), S("LST", 64, 80)
-        vts(S("LST", 48, 64), S("wl", 1, 17), -1.0, float(NONE), ALU.mult, ALU.add, tag="wb")
-        vtt(fw, S("LST", 48, 64), fail, ALU.mult, tag="fw")
+        fail, FR = lst(4), S("FR", 0, 256)
+        vts(fail, S("KEY", 0, 16), col(12), -4096.0, ALU.is_ge, ALU.mult, tag="fail")
+        vts(lst(6), S("oi", 0, 16), float(NONE), None, ALU.is_equal, tag="FL")
+        vtt(lst(5), lst(1), fail, ALU.mult, tag="fw")
         p = reg()
-        bcast(p, fail, 256, "bf")
-        act(S("FR", 0, 256), S(p, 0, 256), ACT.Copy, 0.0, 2.0)
-        firsts("LST", "OR", "I12", "EQo", "ooff", [S(ZO, h * ZW + LH, h * ZW + ZW) for h in range(H)])
-        for h in range(H):
-            vtt(S("tA", h * LH, h * LH + LH), (MTw, S("wu", h * NB, h * NB + NB)), row("OR", h), ALU.not_equal, tag="neM")
-            vtt(S("tA", 256 + h * LH, 256 + h * LH + LH), (NTw, S("ou", h * NB, h * NB + NB)), row("WR", h),
-                ALU.not_equal, tag="neN")
+        bcast(p, fail, "bf")
+        act(FR, S(p, 0, 256), ACT.Copy, 0.0, -2.0 / 4096)
+        rw2 = lambda u, h: row("WR", h) if u else S("OR", h * LH, h * LH + LH)
+        pd, pr = reg(), S(reg(), 0, 32)
+        mm([(S(pd, a, 512, 16), idn("I12"), lst(0, 2)) for a in range(16)], each=1, tag="pd")
+        for u, rw in enumerate(("OR", "WR")):
+            for h in range(H):
+                c, r = 256 * u + h * LH, rw2(u, h)
+                vtt(S("EQ", c, c + LH), S(pd, c, c + LH), r, ALU.is_equal)
+                vtt(S("EQ", 512 + c + 16, 512 + c + LH), S(pd, c, c + LH - 16), S(rw, r[1] + 16, r[2]), ALU.is_equal)
+        mm([(pr, S("Bt", 143 * a + 15, 143 * a + 143), S("EQ", a, 512, 16)) for a in range(16)]
+           + [(S(pr[0], 1, 32, 2), Bw("B1", a), S("EQ", 528 + a, 1024, 32)) for a in range(16)]
+           + [(S(pr[0], 0, 16), idn("Im10"), lst(0)), (S(pr[0], 16, 32), idn("Id"), lst(1)),
+              (S(pr[0], 0, 16), idn("Id"), lst(6))], tag="pr")
+        for u in range(2):
+            vts(S("off", u, 32, 2), S(pr[0], u, 32, 2), 4096.0, col(15 + u), ALU.mult, ALU.min)
+        neM, neN = S("NE", 0, 256), S("NE", 256, 512)
         p = reg()
-        mm([(S(p, 0, 512), idn("I23"), S("tA", 0, 512)), (S(p, 0, 256), idn("I34"), S("FR", 0, 256)),
-            (S(p, 256, 512), idn("I34"), S("FR", 0, 256))], tag="B")
-        act(S("sB", 0, 512), S(p, 0, 512), ACT.Relu)
+        for u in range(2):
+            vtt(lst(2 + u), lst(u), fail, ALU.add, tag="op")
+        bcast(p, lst(2, 2), "bp")
+        for u, pad in enumerate(("EP", "NP")):
+            for h in range(H):
+                c = 256 * u + h * LH
+                vtt(S("NE", c, c + LH), ep(pad, h), S(p, c, c + LH), ALU.not_equal)
+        entries = lambda p, pad: [(S(p, h * LH, h * LH + LH), idn("I12"), ep(pad, h)) for h in range(H)]
         Pm = lambda a: S("Bm", 144 * a + 15 - (a + t) % 16, 144 * a + 143 - (a + t) % 16)
         p = reg()
-        mm([(S(p, 0, 256), idn("nId"), S("sB", 0, 256))]
-           + [(S(p, h * LH, h * LH + LH), idn("nIf"), ep("EP", h)) for h in range(H)], tag="pM")
-        act(S("rM", 0, 256), S(p, 0, 256), ACT.Relu, 4096.0 * NONE)
-        p = reg()
-        mm([(S(p, 0, 256), idn("nId"), S("sB", 256, 512))]
-           + [(S(p, h * LH, h * LH + LH), idn("nIf"), ep("NP", h)) for h in range(H)]
-           + [(S(p, a, 256, 16), Pm(a), fail) for a in range(16)], tag="pN")
-        act(S("rN", 0, 256), S(p, 0, 256), ACT.Relu, float(NONE))
-        p = reg()
+        pA, pB = S(p, 0, 256), S(p, 256, 512)
         if last:
-            act(S("Mo", 0, 256), (MTw, S("ou", 0, 16)), ACT.Copy, 0.0, 4096.0)
-        mm([(S(p, 0, 256), idn("If"), S("Mo", 0, 256))] * last + [(S(p, a, 256, 16), Pm(a), fw) for a in range(16)],
-           each=not last, tag="pQ")
-        act(S("Q", 0, 256), S(p, 0, 256), ACT.Identity, float(NONE), 1.0 / 4096)
-        for b in range(14, -1, -2):
-            vtt((S("MC" if last else "NT", 0, WP), S("ooff", b, b + 2)), S("Q", 16 * b, 16 * b + 32),
-                S("rN", 16 * b, 16 * b + 32), ALU.subtract, tag="scN")
+            act(S("Mo", 0, 256), (MTw, S("ou", 0, 16)), ACT.Relu, TOP, -1.0)
+        mm([(pA, idn("I11"), FR), (pB, idn("Hn"), FR)] + entries(p, "NP") + [(pB, idn("If"), S("Mo", 0, 256))] * last
+           + [(S(p, a, 512, 16), Pm(a), lst(4, 2)) for a in range(16)], stop=False, tag="pN")
+        mm([(pA, idn("nI12"), neN), (pB, idn("H47"), neN)], start=False, tag="qN")
+        act(S("nA", 0, 256), pA, ACT.Relu)
+        act(S("nB", 0, 256), pB, ACT.Identity, TOP * last, -1.0)
+        scatter("MC" if last else "NT", 0, "nA", "nB", ALU.add, "scN")
+        p = S(reg(), 0, 256)
+        mm([(p, idn("I27" if last else "nI27"), FR)] + entries(p[0], "EP") + [(p, idn("nI28" if last else "I28"), neM)], tag="pM")
         if last:
-            p = reg()
-            mm([(S(p, 0, 256), idn("If"), S("rM", 0, 256))]
-               + [(S(p, h * LH, h * LH + LH), idn("If"), ep("EP", h)) for h in range(H)], tag="pD")
-            act(S("dM", 0, 256), S(p, 0, 256), ACT.Identity, -4096.0 * NONE)
+            act(S("rM", 0, 256), p, ACT.Relu, TOP - 2.0 ** 30, -4.0)
             act(S("Yw", 0, 256), (S("MC", 0, W), S("wu", 0, 16)), ACT.Copy)
+            scatter("MC", 16, "Yw", "rM", ALU.add, "scM")
         else:
+            act(S("rM", 0, 256), p, ACT.Relu, FAR, -4.0)
+            if TWO:
+                scatter("ME", 16, "cN", "rM", ALU.subtract, "scE")
+            scatter("MT", 16, "cN", "rM", ALU.subtract, "scM")
             p = reg()
-            for h in range(H):
-                zo, zb = S(ZO, h * ZW, h * ZW + LH), S(ZB, h * ZW, h * ZW + LH)
-                for u in range(2):
-                    o = S(p, 256 * u + h * LH, 256 * u + h * LH + LH)
-                    mm([(o, idn("Id"), zo), (o, idn("nId"), zb),
-                        (o, idn("nId" if u else "Id"), S("FR", h * LH, h * LH + LH))], tag="X1")
-            act(S("rX", 0, 512), S(p, 0, 512), ACT.Relu)
-            p = reg()
-            mm([(S(p, 0, 256), idn("Id"), S("rX", 0, 256)), (S(p, 0, 256), idn("nId"), S("rX", 256, 512)),
-                (S(p, 0, 256), idn("nId"), S("FR", 0, 256))]
-               + [(S(p, h * LH, h * LH + LH), idn("nId"), S(ZO, h * ZW, h * ZW + LH)) for h in range(H)], tag="X2")
-            act(S("x2", 0, 256), S(p, 0, 256), ACT.Identity, 31.0)
-            for b in range(14, -1, -2):
-                vcopy((S("XT", 0, WP), S("ooff", b, b + 2)), S("x2", 16 * b, 16 * b + 32), tag="scX")
+            mm([(S(p, 256 * u, 256 * u + 256), idn(n), s) for u in range(2)
+                for n, s in (("Id", S(ZO, 0, 256)), ("nId" if u else "Id", FR))], each=2, tag="pX")
+            vtt(S("x1", 0, 256), S(ZB, 0, 256), S(p, 0, 256), ALU.min)
+            vtt(S("x2", 0, 256), S("x1", 0, 256), S(p, 256, 512), ALU.max)
+            scatter("XT", 0, "x2", None, None, "scX")
             p = S(reg(), 0, 16)
             mm([(p, idn("ones"), fail)], tag="pS")
             add("V", 64 * CYC, [p], [col(13)],
                 lambda q, R, p=p: q.tensor_reduce(R(col(13)), R(p), AxisListType.X, ALU.add, negate=True), tag="s")
-            vcopy(ci(13), col(13), tag="s")
+            vts(ci(13), col(13), -1.0 / 4096, None, ALU.mult, tag="s")
             vts(ci(14), ci(13), 31, None, AND, tag="s")
             vts(col(12), ci(14), col(11), 32768.0, ALU.add, ALU.mult, tag="s")
-        for b in range(14, -1, -2):
-            u = (16 * b, 16 * b + 32)
-            vtt((S("MC" if last else "MT", 0, WP), S("woff", b, b + 2)), S("Yw", *u) if last else S("cN", 0, 32),
-                S("dM" if last else "rM", *u), ALU.subtract, tag="scM")
     dma("Y", S("ynm", 0, 0), S("MC", 0, W), 3500)
     dma("Y", S("yz", 0, 0), S("ZF", 0, 256), 300)
     dma("Y", S("yw", 0, 0), S("WF", 0, 16), 100)
@@ -404,7 +435,7 @@ def build_ops():
 def find_deps(ops):
     hist = {}
     for i, o in enumerate(ops):
-        d = {i - 1} if 0 < i < 8 else set()
+        d = {i - 1} if 0 < i < NL else set()
         acc = [(s, False) for s in o["rd"]] + [(s, True) for s in o["wr"]] + ([(o["dst"], True)] if "dst" in o else [])
         acc = [(s[0], s[0][0] == "@", w) + ((0, 1 << 20) if s[0][0] == "@" or s[2] == 0 else (s[1], s[2])) for s, w in acc]
         for name, psum, w, lo, hi in acc:
@@ -417,7 +448,7 @@ def find_deps(ops):
                 l[:] = [e for e in l if e[0] == i or not (lo <= e[1] and e[2] <= hi)]
             l.append((i, lo, hi, w))
         o["deps"] = sorted(d)
-        o["wait"] = [j for j in o["deps"] if i >= 8 and (ops[j]["eng"] != "P" or o["eng"] != "P")]
+        o["wait"] = [j for j in o["deps"] if i >= NL and (ops[j]["eng"] != "P" or o["eng"] != "P")]
         o["regs"] = sorted(set(s[0] for s in o["rd"] + o["wr"] if s[0][0] == "@"))
         o["succ"] = []
         for j in o["deps"]:
@@ -519,7 +550,7 @@ def best_plan(ops, tries):
     prio = [0.0] * len(ops)
     for i in range(len(ops) - 1, -1, -1):
         prio[i] = c[i] + ops[i]["lat"] + hop + max([prio[k] for k in ops[i]["succ"]] + [0.0])
-    early = "bf FR B sB pM pN rM rN neM neN Q pQ X1 X2 rX x2 dEQo EQo rEQo ooff fw".split()
+    early = "fail FL op wp fw bf FR pd EQ pr off bp NE pN nA nB pM rM pX x1 x2".split()
     best = schedule(ops, c, [p + 3000 * (o["tag"][-2:] == ".0" or o["tag"] in early) for p, o in zip(prio, ops)], 0, hop)
     bv, tags = value(best), sorted(set(o["tag"] for o in ops))
     for it in range(tries):
@@ -547,7 +578,91 @@ def best_plan(ops, tries):
             v = value(p)
             if v < bv + 1500.0 * max(0.0, 1 - it / (0.8 * tries)) * (rnd(1000) / 1000.0) ** 3:
                 best, bv = p, v
-    return best
+    return polish(ops, best[0], rnd, MOVES)
+
+
+def polish(ops, order, rnd, moves):
+    n = len(ops)
+    eng = ["VSPGY".index(o["eng"]) for o in ops]
+    wait, deps, succ = [o["wait"] for o in ops], [o["deps"] for o in ops], [o["succ"] for o in ops]
+    regs = [o["regs"][0] if o["regs"] else None for o in ops]
+    total = {}
+    for r in regs:
+        total[r] = total.get(r, 0) + 1
+    sets = [(costs(ops, *s[:3]), [o["lat"] * f + s[3] for o in ops], w) for s, w, f in zip(SPEEDS, WEIGHTS, LATS) if w]
+
+    def run(order, cost, lat, extra):
+        free, fin, why, prev = [0.0] * 5, [0.0] * n, [-1] * n, [-1] * 5
+        first = extra is None
+        if first:
+            extra, bank, left, held, rel, use = {}, {}, dict(total), [False] * 8, [0.0] * 8, [[] for _ in range(8)]
+        for i in order:
+            e = eng[i]
+            st, y = free[e], prev[e]
+            for j in wait[i]:
+                if fin[j] > st:
+                    st, y = fin[j], j
+            r = regs[i]
+            if r:
+                if first:
+                    if r not in bank:
+                        b = min([(rel[k], k) for k in range(8) if not held[k]] + [(0, -1)] * all(held))[1]
+                        if b < 0:
+                            return None
+                        bank[r], extra[i], use[b] = b, [j for j in use[b] if eng[j] != 2], []
+                    b = bank[r]
+                    left[r] -= 1
+                    held[b] = left[r] > 0
+                    use[b].append(i)
+                for j in extra.get(i, ()):
+                    if fin[j] > st:
+                        st, y = fin[j], j
+            free[e] = st = st + cost[i]
+            fin[i] = st + lat[i]
+            if r and first:
+                rel[b] = max(rel[b], fin[i])
+            why[i], prev[e] = y, i
+        return max(fin), fin, why, extra, bank if first else None
+
+    def value(order):
+        res = [run(order, sets[0][0], sets[0][1], None)]
+        if res[0] is None:
+            return None
+        res += [run(order, c, l, res[0][3]) for c, l, w in sets[1:]]
+        return sum(r[0] * s[2] for r, s in zip(res, sets)), res
+
+    cur = value(order)
+    best = (cur[0], order, cur[1])
+    for it in range(moves):
+        fin, why = cur[1][rnd(len(sets))][1:3]
+        i, path = fin.index(max(fin)), []
+        while why[i] >= 0:
+            if eng[why[i]] == eng[i] and why[i] not in deps[i]:
+                path.append(i)
+            i = why[i]
+        pos = {k: p for p, k in enumerate(order)}
+        i = path[rnd(len(path))] if path and rnd(8) else rnd(n)
+        mine = [k for k in order[max(0, pos[i] - 120):pos[i]] if eng[k] == eng[i]][-(1, 1, 2, 4, 8, 16)[rnd(6)]:]
+        if not mine:
+            continue
+        p, fwd = mine[0], rnd(2)
+        a, b = pos[p], pos[i]
+        cone, todo = {i if fwd else p}, [i if fwd else p]
+        while todo:
+            for j in (deps if fwd else succ)[todo.pop()]:
+                if j not in cone and a <= pos[j] <= b:
+                    cone.add(j)
+                    todo.append(j)
+        if p in cone and i in cone:
+            continue
+        one, two = [k for k in order[a:b + 1] if k in cone], [k for k in order[a:b + 1] if k not in cone]
+        new = order[:a] + (one + two if fwd else two + one) + order[b + 1:]
+        v = value(new)
+        if v and v[0] <= cur[0] + HEAT * max(0.0, 1 - it / (0.9 * moves)) * (rnd(1000) / 1000.0) ** 2:
+            order, cur = new, v
+            if v[0] < best[0]:
+                best = (v[0], new, v[1])
+    return best[1], best[2][0][4], best[2][0][3], best[2][0][1]
 
 
 OPS = build_ops()

@@ -8,18 +8,20 @@ REP = 4
 KS = (2, 2, 4, 4, 4)
 GREP = True
 TWO = False
+GTF = False
 MS = 1
 XV = ((), (3,))
 XS = 2
-TRIES, MOVES, HEAT = 1200, 40000, 300.0
-WEIGHTS, LATS = (2.0, 0.0, 0.85, 0.8), (1.0, 1.0, 1.3, 1.3)
-SPEEDS = [(1.5, 3.8, 0.42, 110.0), (1.1, 2.0, 0.42, 110.0), (2.0, 5.5, 0.42, 160.0), (1.5, 3.8, 0.6, 200.0)]
+TRIES, MOVES, HEAT = 300, 120000, 400.0
+TURNS, SLACK = 8, 1000.0
+WEIGHTS, LATS = (2.0, 0.0, 1.0, 0.0), (1.0, 1.0, 1.3, 1.3)
+SPEEDS = [(1.5, 3.8, 0.42, 170.0), (1.2, 2.5, 0.42, 110.0), (2.0, 5.5, 0.42, 130.0), (1.5, 3.8, 0.52, 230.0)]
 NB = 16 // H
 LH = 16 * NB
 EW = LH + 32
 TW = 2 * LH + 32
 WP = W + 32
-NL = 9
+NL = 8
 ZP, XN, RB = 35.0, 48.0, 384
 F32, BF, F16, I32, U16 = "float32", "bfloat16", "float16", "int32", "uint16"
 
@@ -39,11 +41,10 @@ SCRATCH = {_n: ("sbuf", [128, _c], _d) for _n, _c, _d in [
     ("eoff", 256, U16), ("uoff", 256, U16), ("ETf", 256, F16), ("UTf", 256, F16),
     ("WR", REP * 256, F32), ("OR", 256, F32), ("FR", 256, BF),
     ("EQN", 4096, BF), ("XG", 4096, BF), ("AD", 4096, BF), ("EQM", 4096, BF), ("MG", 4096, F16),
-    ("SG", 256, BF), ("SG2", 256, BF), ("CT", 256, BF), ("RUN", 64 * H, F32), ("RUN2", 64 * H, F32),
-    ("TR", 64 * H, F32), ("TR2", 64 * H, F32),
+    ("SG", 256, BF), ("SG2", 256, BF), ("CT", 256, BF), ("cap", NB, BF),
     ("EQ", 1024, BF), ("off", 32, U16), ("NE", 512, F16), ("rM", 256, F32), ("nA", 256, F32), ("nB", 256, F32),
     ("Mo", 256, F32), ("Yw", 256, F32), ("x1", 256, BF), ("x2", 256, BF),
-    ("WI0", 64 * H, I32), ("WI1", 64 * H, I32), ("WI2", 64 * H, I32), ("WF", 16, F32),
+    ("WI0", 16, I32), ("WI1", 16, I32), ("WI2", 16, I32), ("WF", 16, F32),
     ("WO0", 16, I32), ("WO1", 16, I32), ("WOF", 16, F32),
     ("ZB0", 256, BF), ("ZB1", 256, BF), ("ZB2", 256, BF), ("ZF", 256, BF),
     ("ZO0", 256, BF), ("ZO1", 256, BF), ("ZO2", 256, BF)]}
@@ -144,7 +145,7 @@ def build_ops():
         add(eng, 1000 if acc else 60, [in_], [out], lambda q, R: q.dma_start(R(out), R(in_), **kw), lat=1900 + lat, kind="d")
 
     def send(dst, src, nbytes):
-        add("G", 300, [src], [], None, lat=2200 + nbytes / 100.0, kind="r").update({"dst": dst, "src": src})
+        add("G", 900, [src], [], None, lat=2200 + nbytes / 60.0, kind="r").update({"dst": dst, "src": src})
 
     col = lambda j: S("col", j, j + 1)
     ci = lambda j: S("coli", j, j + 1)
@@ -156,12 +157,11 @@ def build_ops():
     FAR = TOP + 2.0 ** 29
     AND, SHR = ALU.bitwise_and, ALU.arith_shift_right
 
-    for h in range(H):
-        dma("Y", S("WI0", 64 * h, 64 * h + NB), S("w", h * NB, h * NB + NB), 100)
+    dma("Y", S("WI0", 0, 16), S("w", 0, 0), 100)
     for c in range(4):
         dma("Y", S("nmi", 512 * c, 512 * c + 512), S("nm", 512 * c, 512 * c + 512), 870 * (c + 1))
-    dma("Y", S("ZB0", 0, 256), S("z", 0, 0), 3600)
-    dma("Y", XTw, S("x", 0, 0), 5200)
+    dma("Y", XTw, S("x", 0, 0), 5000)
+    dma("Y", S("ZB0", 0, 256), S("z", 0, 0), 5200)
     dma("Y", S("thi", 0, 1), S("th", 0, 0), 5200)
     giota(ci(0), [[0, 1]], 0, 1)
     vset(S("ones", 0, 576), 1.0)
@@ -179,7 +179,7 @@ def build_ops():
     for n, v in (("nId", -1.0), ("I12", 4096.0), ("nI12", -4096.0), ("I11", 2048.0), ("IR", -RB * 32768.0),
                  ("Im10", 1.0 / 1024), ("I15", 32768.0), ("nI27", -2.0 ** 27), ("I28", 2.0 ** 28), ("If", 1.0),
                  ("I27", 2.0 ** 27), ("nI28", -2.0 ** 28), ("H47", -float(NONE)), ("Hn", NONE / 2.0)):
-        act(idn(n), idn("Id"), ACT.Copy, 0.0, v)
+        vts(idn(n), idn("Id"), v, None, ALU.mult)
     vts(S("KC", 0, LH), S("KF", 0, LH), (RB - 512) * 16.0, None, ALU.add)
     vcopy(S("KC", LH, 2 * LH), S("KF", 0, LH))
     vts(ci(1), ci(0), 15, None, AND)
@@ -195,9 +195,9 @@ def build_ops():
     act(S("Ie12", 0, 256), S("Ie", 0, 256), ACT.Copy, 0.0, 1024.0)
     vset(S("EP", 0, H * EW), 0.0)
     vset(S("NP", 0, H * EW), 0.0)
-    for t in range(RO):
-        for h in range(H):
-            vset(S("WI%d" % t, 64 * h + NB, 64 * h + 64), 2 ** 24)
+    vts(col(5), S("Id", 0, 1), 2.0 ** 24, None, ALU.mult)
+    vtt(col(6), col(5), S("Id", 1, 2), ALU.subtract)
+    vts(S("cap", 0, NB), S("ones", 0, NB), col(6), None, ALU.mult)
     vset(S("cN", 0, 32), FAR)
     vts(col(11), S("thi", 0, 1), -512.0, None, ALU.add)
     vts(col(12), col(11), 32768.0, None, ALU.mult)
@@ -237,7 +237,10 @@ def build_ops():
         mm([(S(p, b, LH, NB), idn(mask, u), S(tr, src(b, u), src(b, u) + 16)) for b in range(NB) for u in range(2)],
            each=2, tag="t" + off)
         vts(S(off, h * LH, h * LH + LH), S(p, 0, LH), float(NONE), None, ALU.min)
-        vcopy(S(tf, h * LH, h * LH + LH), S(off, h * LH, h * LH + LH))
+        if GTF:
+            gsel(S(tf, h * LH, h * LH + LH), S(off, h * LH, h * LH + LH), [[0, LH]], ALU.is_ge, 0, 0)
+        else:
+            vcopy(S(tf, h * LH, h * LH + LH), S(off, h * LH, h * LH + LH))
 
     def compare(h, out, win, off, rw):
         k = 0
@@ -247,31 +250,28 @@ def build_ops():
                 ALU.is_equal, tag=out + str(k * NB // 64))
             k += n
 
-    def keys(h, eq, val, sg, tf, kc, run, tr, first, key):
-        for c in range(LH // 64):
-            d0, k0, u = h * 16 * LH + 1024 * c, h * LH + 64 * c, val + str(c)
-            pc, pk = S(reg(), 0, 64), S(reg(), 0, 64)
+    def keys(h, eq, val, sg, tf, kc, run, first, key):
+        p, q, n, h0 = reg(), reg(), reg(), h * LH
+        low = [(S(p, 0, LH), idn("I11"), S("KC", kc, kc + LH)), (S(p, 0, LH), idn("Id"), S(tf, h0, h0 + LH)),
+               (S(p, LH, LH + NB),) + first]
+        for c in range(2):
+            d0, k0, u = h * 16 * LH + 1024 * c, h0 + 64 * c, val + str(c)
+            pc, pk = S(q, 64 * c, 64 * c + 64), S(p, 64 * c, 64 * c + 64)
             mm([(pc, Bw("B1", a), S(eq, d0 + a, d0 + 1024, 16)) for a in range(16)], tag="C" + u)
-            act(S(sg, k0, k0 + 64), pc, ACT.Sign)
-            low = [(pk, idn("I11"), S("KC", kc + 64 * c, kc + 64 * c + 64)), (pk, idn("Id"), S(tf, k0, k0 + 64))]
-            flag = [(pk, idn("IR"), S(sg, k0, k0 + 64))]
-            if first is None:
-                mm(low + [(pk, Bw("B15", a), S(val, d0 + a, d0 + 1024, 16)) for a in range(16)], stop=False, tag="K" + u)
-                mm(flag, start=False, tag="L" + val)
+            if kc == 0:
+                mm(low * (1 - c) + [(pk, Bw("B15", a), S(val, d0 + a, d0 + 1024, 16)) for a in range(16)],
+                   start=c == 0, stop=False, tag="K" + u)
             else:
-                pn = S(reg(), 0, 64)
-                mm([(pn, Bw("B1", a), S(val, d0 + a, d0 + 1024, 16)) for a in range(16)], tag="K" + u)
-                act(S("CT", k0, k0 + 64), pn, ACT.Identity, 192.0, -1.0 / 32768)
-                mm(low + [(pk, idn("I15"), S("CT", k0, k0 + 64))] + flag, tag="L" + val)
-            r = S(run, 64 * h, 64 * h + 64)
-            if c == 0 and first is None:
-                vts(r, pk, 2.0 ** 24 - 1, None, ALU.min)
-            else:
-                vtt(r, pk, r if c else first, ALU.min)
-        n, src, a, to = 32, run, 64 * h, 64 * h
-        while n >= NB:
-            vtt(key if n == NB else S(tr, to, to + n), S(src, a, a + n), S(src, a + n, a + 2 * n), ALU.min, tag=run)
-            src, a, to, n = tr, to, to + n, n // 2
+                mm([(S(n, 64 * c, 64 * c + 64), Bw("B1", a), S(val, d0 + a, d0 + 1024, 16)) for a in range(16)], tag="K" + u)
+        act(S(sg, h0, h0 + LH), S(q, 0, LH), ACT.Sign)
+        if kc:
+            act(S("CT", h0, h0 + LH), S(n, 0, LH), ACT.Identity, 192.0, -1.0 / 32768)
+        pk = S(p, 0, LH)
+        mm((low + [(pk, idn("I15"), S("CT", h0, h0 + LH))] if kc else []) + [(pk, idn("IR"), S(sg, h0, h0 + LH))],
+           start=kc > 0, tag="L" + val)
+        for b in range(NB):
+            i, o = S(p, b, LH + NB, NB), S(key, h * NB + b, h * NB + b + 1)
+            add("V", 64 * CYC, [i], [o], lambda q, R, i=i, o=o: q.tensor_reduce(R(o), R(i), AxisListType.X, ALU.min), tag=run)
 
     def scatter(table, o0, a, b, op, tag):
         for k in range(14, -1, -2):
@@ -293,7 +293,7 @@ def build_ops():
         for h in range(H):
             at[0] = "." + str(h)
             b0, b1, l0, d0 = h * NB, h * NB + NB, h * LH, h * 16 * LH
-            zb, wi = S(ZB, l0, l0 + LH), S(WI, 64 * h, 64 * h + NB)
+            zb, wi = S(ZB, l0, l0 + LH), S(WI, b0, b1)
             vcopy(S("wu", b0, b1), wi)
             vts(S("LST", 16 + b0, 16 + b1), wi, 1.0 / 4096, None, ALU.mult, tag="ws")
             if t:
@@ -321,7 +321,7 @@ def build_ops():
                 p = reg()
                 mm([(S(p, 0, 512), idn("Id"), xg)] + [(S(p, k * LH, k * LH + LH), idn("nId"), zb) for k in range(kp)], tag="xP")
                 act(ad, S(p, 0, 512), ACT.Abs, tag="AD%d" % c)
-            keys(h, "EQN", "AD", "SG", "ETf", 0, "RUN", "TR", None, S("KEY", b0, b1))
+            keys(h, "EQN", "AD", "SG", "ETf", 0, "RUN", (idn("ones"), S("cap", 0, NB)), "KEY")
             vts(S("oi", b0, b1), S("KEY", b0, b1), NONE, None, AND)
             vcopy(S("ou", b0, b1), S("oi", b0, b1))
             vts(S("LST", b0, b1), S("oi", b0, b1), 0.25, None, ALU.mult, tag="ol")
@@ -344,29 +344,27 @@ def build_ops():
                 act(zo, (XTw, S("ou", b0, b1)), ACT.Copy, tag="xo")
             else:
                 vts(zo, (XTw, S("ou", b0, b1)), ZP, None, ALU.min, tag="xo")
-            send(S("ZF" if last else "ZB%d" % (t + 1), l0, l0 + LH), zo, 256 * LH)
+            if h == H - 1:
+                send(S("ZF" if last else "ZB%d" % (t + 1), 0, 256), S(ZO, 0, 256), 256 * 256)
             for c in range(0, 4, MS):
                 act(S("MG", d0 + 512 * c, d0 + 512 * (c + MS)), (MTw, S("uoff", l0 + 32 * c, l0 + 32 * (c + MS))),
                     ACT.Copy, 0.0, 2.0 ** -14, tag="MG%d" % (c // 2))
             for c in range(4):
                 d = d0 + 512 * c
                 vtt(S("EQM", d, d + 512), S("MG", d, d + 512), S(po, 0, 512), ALU.is_equal, tag="EQM%d" % (c // 2))
-            keys(h, "EQM", "MG", "SG2", "UTf", LH, "RUN2", "TR2", S(WI, 64 * h, 64 * h + 64), S("KEY2", b0, b1))
+            keys(h, "EQM", "MG", "SG2", "UTf", LH, "RUN2", (idn("I12"), S("LST", 16 + b0, 16 + b1)), "KEY2")
             if last:
                 vts(S("wand", b0, b1), S("KEY2", b0, b1), NONE, None, AND)
                 vcopy(S("WOF", b0, b1), S("wand", b0, b1))
                 send(S("WF", b0, b1), S("WOF", b0, b1), 512 * NB)
             else:
                 vts(S("WO%d" % t, b0, b1), S("KEY2", b0, b1), NONE, None, AND, tag="wand")
-                send(S("WI%d" % (t + 1), 64 * h, 64 * h + NB), S("WO%d" % t, b0, b1), 512 * NB)
+                send(S("WI%d" % (t + 1), b0, b1), S("WO%d" % t, b0, b1), 512 * NB)
         at[0] = ""
         fail, FR = lst(4), S("FR", 0, 256)
         vts(fail, S("KEY", 0, 16), col(12), -4096.0, ALU.is_ge, ALU.mult, tag="fail")
         vts(lst(6), S("oi", 0, 16), float(NONE), None, ALU.is_equal, tag="FL")
         vtt(lst(5), lst(1), fail, ALU.mult, tag="fw")
-        p = reg()
-        bcast(p, fail, "bf")
-        act(FR, S(p, 0, 256), ACT.Copy, 0.0, -2.0 / 4096)
         rw2 = lambda u, h: row("WR", h) if u else S("OR", h * LH, h * LH + LH)
         pd, pr = reg(), S(reg(), 0, 32)
         mm([(S(pd, a, 512, 16), idn("I12"), lst(0, 2)) for a in range(16)], each=1, tag="pd")
@@ -386,6 +384,7 @@ def build_ops():
         for u in range(2):
             vtt(lst(2 + u), lst(u), fail, ALU.add, tag="op")
         bcast(p, lst(2, 2), "bp")
+        act(FR, S(p, 256, 512), ACT.Relu, 0.0, -2.0 / 4096)
         for u, pad in enumerate(("EP", "NP")):
             for h in range(H):
                 c = 256 * u + h * LH
@@ -578,7 +577,9 @@ def best_plan(ops, tries):
             v = value(p)
             if v < bv + 1500.0 * max(0.0, 1 - it / (0.8 * tries)) * (rnd(1000) / 1000.0) ** 3:
                 best, bv = p, v
-    return polish(ops, best[0], rnd, MOVES)
+    for e in range(TURNS):
+        best = refine(ops, banks(ops, best), rnd, MOVES // TURNS, HEAT * (1 - e / TURNS), HEAT * (1 - (e + 1) / TURNS))
+    return best
 
 
 def polish(ops, order, rnd, moves):
@@ -631,6 +632,12 @@ def polish(ops, order, rnd, moves):
         res += [run(order, c, l, res[0][3]) for c, l, w in sets[1:]]
         return sum(r[0] * s[2] for r, s in zip(res, sets)), res
 
+    seen, kin = {}, {}
+    for i, o in enumerate(ops):
+        k = (o["tag"], o["eng"], o["t"])
+        seen[k] = seen.get(k, 0) + 1
+        kin.setdefault((o["tag"], o["eng"], seen[k]), []).append(i)
+    twins = {i: l for l in kin.values() for i in l}
     cur = value(order)
     best = (cur[0], order, cur[1])
     for it in range(moves):
@@ -640,9 +647,150 @@ def polish(ops, order, rnd, moves):
             if eng[why[i]] == eng[i] and why[i] not in deps[i]:
                 path.append(i)
             i = why[i]
-        pos = {k: p for p, k in enumerate(order)}
-        i = path[rnd(len(path))] if path and rnd(8) else rnd(n)
-        mine = [k for k in order[max(0, pos[i] - 120):pos[i]] if eng[k] == eng[i]][-(1, 1, 2, 4, 8, 16)[rnd(6)]:]
+        i = path[rnd(len(path))] if path and rnd(6) else rnd(n)
+        fwd = rnd(2)
+        if rnd(2):
+            key = [f - c - l for f, c, l in zip(cur[1][0][1], sets[0][0], sets[0][1])]
+            i = i if fwd or why[i] < 0 else why[i]
+            far, d = (0, 700, 2000, 5000)[rnd(4)], (120, 300, 700, 1500, 3000)[rnd(5)]
+            todo = list(twins[i]) if rnd(2) else [i]
+            cone = {k: key[k] for k in todo}
+            while todo:
+                k = todo.pop()
+                for j in (deps if fwd else succ)[k]:
+                    if j not in cone and abs(key[j] - cone[k]) < far:
+                        cone[j] = cone[k]
+                        todo.append(j)
+            for k in cone:
+                key[k] += -d if fwd else d
+            for k in range(n):
+                for j in deps[k]:
+                    if key[j] >= key[k]:
+                        key[k] = key[j] + 0.01
+            new = sorted(range(n), key=lambda k: key[k])
+        else:
+            pos = {k: p for p, k in enumerate(order)}
+            mine = [k for k in order[max(0, pos[i] - 120):pos[i]] if eng[k] == eng[i]][-(1, 1, 2, 4, 8, 16)[rnd(6)]:]
+            if not mine:
+                continue
+            p = mine[0]
+            a, b = pos[p], pos[i]
+            cone, todo = {i if fwd else p}, [i if fwd else p]
+            while todo:
+                for j in (deps if fwd else succ)[todo.pop()]:
+                    if j not in cone and a <= pos[j] <= b:
+                        cone.add(j)
+                        todo.append(j)
+            if p in cone and i in cone:
+                continue
+            one, two = [k for k in order[a:b + 1] if k in cone], [k for k in order[a:b + 1] if k not in cone]
+            new = order[:a] + (one + two if fwd else two + one) + order[b + 1:]
+        v = value(new)
+        if v and v[0] <= cur[0] + HEAT * max(0.0, 1 - it / (0.9 * moves)) * (rnd(1000) / 1000.0) ** 2:
+            order, cur = new, v
+            if v[0] < best[0]:
+                best = (v[0], new, v[1])
+    return best[1], best[2][0][4], best[2][0][3], best[2][0][1]
+
+
+def banks(ops, plan):
+    left, bank, rel, held = {}, {}, [0.0] * 8, [False] * 8
+    for o in ops:
+        for r in o["regs"]:
+            left[r] = left.get(r, 0) + 1
+    for i in plan[0]:
+        for r in ops[i]["regs"]:
+            if r not in bank:
+                bank[r] = min((held[b], rel[b], b) for b in range(8))[2]
+            left[r] -= 1
+            held[bank[r]], rel[bank[r]] = left[r] > 0, max(rel[bank[r]], plan[3][i])
+    return plan[0], bank
+
+
+def refine(ops, plan, rnd, moves, hot, cold):
+    n, order, bank = len(ops), list(plan[0]), plan[1]
+    eng = ["VSPGY".index(o["eng"]) for o in ops]
+    sets = [(costs(ops, *s[:3]), [o["lat"] * f + s[3] for o in ops], w) for s, w, f in zip(SPEEDS, WEIGHTS, LATS) if w]
+    use, held, deps, wait, extra = {}, {}, [list(o["deps"]) for o in ops], [list(o["wait"]) for o in ops], {}
+    for i in order:
+        for r in ops[i]["regs"]:
+            b = bank[r]
+            if held.get(b) != r:
+                extra[i] = [j for j in use.get(b, []) if eng[j] != 2]
+                deps[i] += use.get(b, [])
+                wait[i] += extra[i]
+                use[b], held[b] = [], r
+            use[b].append(i)
+    succ, after = [[] for _ in ops], [[] for _ in ops]
+    for i in range(n):
+        for j in deps[i]:
+            succ[j].append(i)
+        for j in wait[i]:
+            after[j].append(i)
+
+    def paths(order):
+        out = []
+        for cost, lat, w in sets:
+            free, end, tail, why, prev = [0.0] * 5, [0.0] * n, [0.0] * n, [-1] * n, [-1] * 5
+            for i in order:
+                e = eng[i]
+                st, y = free[e], prev[e]
+                for j in wait[i]:
+                    if end[j] + lat[j] > st:
+                        st, y = end[j] + lat[j], j
+                free[e] = end[i] = st + cost[i]
+                why[i], prev[e] = y, i
+            free = [0.0] * 5
+            for i in order[::-1]:
+                x = max([tail[k] for k in after[i]] + [0.0]) + lat[i]
+                free[eng[i]] = tail[i] = max(x, free[eng[i]]) + cost[i]
+            out.append((end, tail, why, max(tail)))
+        return out
+
+    def through(win, a, b):
+        before, behind, res = {}, {}, []
+        for k in range(a - 1, max(-1, a - 200), -1):
+            before.setdefault(eng[order[k]], order[k])
+            if len(before) > 3:
+                break
+        for k in range(b + 1, min(n, b + 200)):
+            behind.setdefault(eng[order[k]], order[k])
+            if len(behind) > 3:
+                break
+        for (cost, lat, w), (end, tail, why, top) in zip(sets, cur):
+            free, new, m = {e: end[k] for e, k in before.items()}, {}, 0.0
+            for i in win:
+                st = free.get(eng[i], 0.0)
+                for j in wait[i]:
+                    x = new.get(j, end[j]) + lat[j]
+                    if x > st:
+                        st = x
+                free[eng[i]] = new[i] = st = st + cost[i]
+                x = 0.0
+                for k in after[i]:
+                    if pos[k] > b and tail[k] > x:
+                        x = tail[k]
+                if st + lat[i] + x > m:
+                    m = st + lat[i] + x
+            for e, k in behind.items():
+                m = max(m, free.get(e, 0.0) + tail[k])
+            res.append(m)
+        return res
+
+    worth = lambda c: sum(x[3] * s[2] for x, s in zip(c, sets))
+    cur = paths(order)
+    best, path = (worth(cur), order), None
+    for it in range(moves):
+        if path is None:
+            pos, path = {k: p for p, k in enumerate(order)}, []
+            for end, tail, why, top in cur:
+                i = end.index(max(end))
+                while why[i] >= 0:
+                    if eng[why[i]] == eng[i] and why[i] not in deps[i]:
+                        path.append(i)
+                    i = why[i]
+        i = path[rnd(len(path))] if path and rnd(4) else rnd(n)
+        mine = [k for k in order[max(0, pos[i] - 90):pos[i]] if eng[k] == eng[i]][-(1, 1, 2, 3, 5, 8, 14)[rnd(7)]:]
         if not mine:
             continue
         p, fwd = mine[0], rnd(2)
@@ -655,14 +803,20 @@ def polish(ops, order, rnd, moves):
                     todo.append(j)
         if p in cone and i in cone:
             continue
-        one, two = [k for k in order[a:b + 1] if k in cone], [k for k in order[a:b + 1] if k not in cone]
-        new = order[:a] + (one + two if fwd else two + one) + order[b + 1:]
-        v = value(new)
-        if v and v[0] <= cur[0] + HEAT * max(0.0, 1 - it / (0.9 * moves)) * (rnd(1000) / 1000.0) ** 2:
-            order, cur = new, v
-            if v[0] < best[0]:
-                best = (v[0], new, v[1])
-    return best[1], best[2][0][4], best[2][0][3], best[2][0][1]
+        old = order[a:b + 1]
+        one, two = [k for k in old if k in cone], [k for k in old if k not in cone]
+        win = one + two if fwd else two + one
+        d = sum(s[2] * (max(x, c[3] - SLACK) - max(y, c[3] - SLACK))
+                for x, y, c, s in zip(through(win, a, b), through(old, a, b), cur, sets))
+        if d <= (hot + (cold - hot) * it / moves) * (rnd(1000) / 1000.0) ** 3:
+            order = order[:a] + win + order[b + 1:]
+            cur, path = paths(order), None
+            if rnd(8) == 0:
+                order.sort(key=lambda k: cur[0][0][k] - sets[0][0][k])
+            if worth(cur) < best[0]:
+                best = (worth(cur), order)
+    cur = paths(best[1])
+    return best[1], bank, extra, [e + l for e, l in zip(cur[0][0], sets[0][1])]
 
 
 OPS = build_ops()

from concourse.mybir import AluOpType, AxisListType, ActivationFunctionType

ALU = AluOpType
ACT = ActivationFunctionType
RO, NR, W, NONE = 3, 8, 2048, 2047
H = 2
REP = 4
KS = (2, 2, 4, 4, 4)
GREP = True
TWO = False
GTF = False
MS = 1
XV = ((), (3,))
XS = 2
TRIES, MOVES, HEAT = 300, 120000, 400.0
TURNS, SLACK = 8, 1000.0
WEIGHTS, LATS = (2.0, 0.0, 1.0, 0.0), (1.0, 1.0, 1.3, 1.3)
SPEEDS = [(1.5, 3.8, 0.42, 170.0), (1.2, 2.5, 0.42, 110.0), (2.0, 5.5, 0.42, 130.0), (1.5, 3.8, 0.52, 230.0)]
NB = 16 // H
LH = 16 * NB
EW = LH + 32
TW = 2 * LH + 32
WP = W + 32
NL = 8
ZP, XN, RB = 35.0, 48.0, 384
F32, BF, F16, I32, U16 = "float32", "bfloat16", "float16", "int32", "uint16"

SCRATCH = {_n: ("sbuf", [128, _c], _d) for _n, _c, _d in [
    ("nmi", W, I32), ("NI", W, I32), ("NT", WP, F32), ("MT", WP, F32), ("ME", WP, F32), ("MC", WP, F32), ("XT", WP, BF),
    ("thi", 4, I32), ("col", 32, F32), ("coli", 32, I32),
    ("ones", 576, BF), ("Sel", 2048, BF), ("Bm", 2304, BF), ("Bt", 2304, BF),
    ("B1", 144, BF), ("B15", 144, BF), ("B0", 144, BF),
    ("Id", 128, BF), ("nId", 128, BF), ("I12", 128, BF), ("nI12", 128, BF), ("I11", 128, BF), ("nI11", 128, BF),
    ("IR", 128, BF), ("Im10", 128, BF), ("I15", 128, BF), ("nI27", 128, BF), ("I28", 128, BF),
    ("I27", 128, BF), ("nI28", 128, BF),
    ("Ie", 256, BF), ("Ie12", 256, BF), ("If", 128, F32), ("rp", 2, U16), ("o4", 32 * H, F16), ("E0", 256, I32),
    ("H47", 128, F16), ("Hn", 128, F16), ("KF", LH, F32), ("KC", 2 * LH, F16), ("cN", 32, F32),
    ("wu", 16, U16), ("ou", 16, U16), ("LST", 112, F16),
    ("KEY", 16, I32), ("oi", 16, I32), ("KEY2", 16, I32), ("wand", 16, I32),
    ("EP", H * EW, F16), ("NP", H * EW, F16), ("TE", H * TW, F16), ("TN", H * TW, F16),
    ("eoff", 256, U16), ("uoff", 256, U16), ("ETf", 256, F16), ("UTf", 256, F16),
    ("WR", REP * 256, F32), ("OR", 256, F32), ("FR", 256, BF),
    ("EQN", 4096, BF), ("XG", 4096, BF), ("AD", 4096, BF), ("EQM", 4096, BF), ("MG", 4096, F16),
    ("SG", 256, BF), ("SG2", 256, BF), ("CT", 256, BF), ("cap", NB, BF),
    ("EQ", 1024, BF), ("off", 32, U16), ("NE", 512, F16), ("rM", 256, F32), ("nA", 256, F32), ("nB", 256, F32),
    ("Mo", 256, F32), ("Yw", 256, F32), ("x1", 256, BF), ("x2", 256, BF),
    ("WI0", 16, I32), ("WI1", 16, I32), ("WI2", 16, I32), ("WF", 16, F32),
    ("WO0", 16, I32), ("WO1", 16, I32), ("WOF", 16, F32),
    ("ZB0", 256, BF), ("ZB1", 256, BF), ("ZB2", 256, BF), ("ZF", 256, BF),
    ("ZO0", 256, BF), ("ZO1", 256, BF), ("ZO2", 256, BF)]}
for _i in range(8):
    SCRATCH["ps%d" % _i] = ("psum", [128, 512], F32)

CYC = 0.83


def S(name, a, b, st=1):
    return (name, a, b, st)


def _n(s):
    return (s[2] - s[1] + s[3] - 1) // s[3]


def _two(*ss):
    return all(len(s) == 4 and s[0][0] != "@" and SCRATCH[s[0]][2] not in (F32, I32) for s in ss)


def build_ops():
    ops, nreg, at = [], [0], ["", 0]

    def reg():
        nreg[0] += 1
        return "@%d" % nreg[0]

    def add(eng, cost, rd, wr, fn, lat=0.0, kind="c", tag="", ge=0, se=0):
        ops.append({"eng": eng, "fix": cost, "ge": ge, "se": se, "rd": rd, "wr": wr, "fn": fn, "lat": lat, "kind": kind,
                    "tag": (tag or (wr or rd)[0][0]) + at[0], "t": at[1]})
        return ops[-1]

    def opnd(R, s):
        if not isinstance(s, tuple):
            return s
        return R(s[0]).indirect(R(s[1])) if len(s) == 2 else R(s)

    def flat(*ss):
        out = []
        for s in ss:
            if isinstance(s, tuple):
                out += list(s) if len(s) == 2 else [s]
        return out

    def vec(out, ins, per, fn, tag):
        if len(out) == 2:
            add("V", 50, [out[1]] + flat(*ins), [out[0]], fn, tag=tag, se=_n(ins[0]))
        elif len(ins[0]) == 2:
            add("V", 50, flat(*ins), [out], fn, tag=tag, ge=_n(out))
        else:
            add("V", max(64, per * _n(ins[0])) * CYC, flat(*ins), [out], fn, tag=tag)

    def vcopy(out, in_, tag=""):
        vec(out, [in_], 0.5 if _two(out, in_) else 1, lambda q, R: q.tensor_copy(opnd(R, out), opnd(R, in_)), tag)

    def vts(out, in_, s1, s2, o0, o1=None, tag=""):
        more = [] if o1 is None else [o1]
        vec(out, [in_, s1, s2], 0.5 if _two(out, in_) else 1,
            lambda q, R: q.tensor_scalar(R(out), opnd(R, in_), opnd(R, s1), opnd(R, s2), o0, *more), tag)

    def vtt(out, a, b, op, tag=""):
        vec(out, [a, b], 1 if a[0][0] == "@" or b[0][0] == "@" else 2,
            lambda q, R: q.tensor_tensor(opnd(R, out), opnd(R, a), R(b), op), tag)

    def vset(out, c):
        add("V", max(64, _n(out) * (0.5 if _two(out) else 1)) * CYC, [], [out], lambda q, R: q.memset(R(out), c))

    def vtr(out, in_):
        vec(out, [in_], 0.5 if _two(out, in_) else 1, lambda q, R: q.transpose(R(out), R(in_)), "")

    def act(out, in_, f, bias=0.0, scale=1.0, tag=""):
        ind = len(in_) == 2
        add("S", 65 + (0 if ind else CYC * _n(out)), flat(in_, bias, scale), [out],
            lambda q, R: q.activation(R(out), opnd(R, in_), f, opnd(R, bias), opnd(R, scale)), tag=tag, ge=_n(out) if ind else 0)

    def mm(lst, start=True, stop=True, each=0, tag=""):
        c = sum(max(64, _n(r)) * (4 if SCRATCH[r[0]][2] == F32 else 1) for o, l, r in lst)

        def fn(q, R):
            ins = None
            for i, (o, l, r) in enumerate(lst):
                a, b = (i % each == 0, i % each == each - 1) if each else (start and i == 0, stop and i == len(lst) - 1)
                ins = q.matmul(R(o), R(l), R(r), a, b)
            return ins
        add("P", c + 64, [x[1] for x in lst] + [x[2] for x in lst], [x[0] for x in lst], fn, tag=tag)

    def gsel(out, in_, pat, op, base, cm, tag=""):
        add("G", 170 + 2 * CYC * _n(out), [in_], [out],
            lambda q, R: q.affine_select(R(out), R(in_), pat, op, 0.0, base, cm), tag=tag)

    def giota(out, pat, base, cm):
        kw = {} if SCRATCH[out[0]][2] == I32 else {"allow_small_or_imprecise_dtypes": True}
        add("G", 130 + 2 * CYC * _n(out), [], [out], lambda q, R: q.iota(R(out), pat, base, cm, **kw))

    def dma(eng, out, in_, lat, acc=False):
        kw = {"accum_op": ALU.add} if acc else {}
        add(eng, 1000 if acc else 60, [in_], [out], lambda q, R: q.dma_start(R(out), R(in_), **kw), lat=1900 + lat, kind="d")

    def send(dst, src, nbytes):
        add("G", 900, [src], [], None, lat=2200 + nbytes / 60.0, kind="r").update({"dst": dst, "src": src})

    col = lambda j: S("col", j, j + 1)
    ci = lambda j: S("coli", j, j + 1)
    idn = lambda n, a=0: S(n, 128 * a, 128 * a + 128)
    Bw = lambda n, a: S(n, 15 - a, 143 - a)
    lst = lambda j, n=1: S("LST", 16 * j, 16 * (j + n))
    NTw, MTw, XTw = S("NT", 0, W), S("MT", 0, W), S("XT", 0, W)
    BIG, TOP = 1.5 * 2.0 ** 35, 4096.0 * NONE
    FAR = TOP + 2.0 ** 29
    AND, SHR = ALU.bitwise_and, ALU.arith_shift_right

    dma("Y", S("WI0", 0, 16), S("w", 0, 0), 100)
    for c in range(4):
        dma("Y", S("nmi", 512 * c, 512 * c + 512), S("nm", 512 * c, 512 * c + 512), 870 * (c + 1))
    dma("Y", XTw, S("x", 0, 0), 5000)
    dma("Y", S("ZB0", 0, 256), S("z", 0, 0), 5200)
    dma("Y", S("thi", 0, 1), S("th", 0, 0), 5200)
    giota(ci(0), [[0, 1]], 0, 1)
    vset(S("ones", 0, 576), 1.0)
    gsel(idn("Id"), idn("ones"), [[-1, 128]], ALU.is_equal, 0, 1)
    for a in range(0, 16, 4):
        gsel(S("Sel", 128 * a, 128 * a + 512), S("ones", 0, 512), [[-1, 4], [-16, 8], [0, 16]], ALU.is_equal, -a, 1)
    gsel(S("B0", 0, 144), S("ones", 0, 144), [[-16, 9], [256, 16]], ALU.is_ge, -256 * 15, 1)
    gsel(S("B1", 0, 144), S("B0", 0, 144), [[16, 9], [0, 16]], ALU.is_ge, 15, -1)
    giota(S("KF", 0, LH), [[1, 16], [0, NB]], 0, 0)
    for a in range(0, 16, 4):
        gsel(S("Bm", 144 * a, 144 * a + 576), S("ones", 0, 576), [[-1, 4], [-16, 9], [256, 16]], ALU.is_equal, -256 * 15 - a, 1)
    for a in range(16):
        gsel(S("Bt", 144 * a, 144 * a + 144), S("B0", 0, 144), [[16, 9], [0, 16]], ALU.is_ge, a - 1, -1)
    act(S("B15", 0, 144), S("B1", 0, 144), ACT.Copy, 0.0, 32768.0)
    for n, v in (("nId", -1.0), ("I12", 4096.0), ("nI12", -4096.0), ("I11", 2048.0), ("IR", -RB * 32768.0),
                 ("Im10", 1.0 / 1024), ("I15", 32768.0), ("nI27", -2.0 ** 27), ("I28", 2.0 ** 28), ("If", 1.0),
                 ("I27", 2.0 ** 27), ("nI28", -2.0 ** 28), ("H47", -float(NONE)), ("Hn", NONE / 2.0)):
        vts(idn(n), idn("Id"), v, None, ALU.mult)
    vts(S("KC", 0, LH), S("KF", 0, LH), (RB - 512) * 16.0, None, ALU.add)
    vcopy(S("KC", LH, 2 * LH), S("KF", 0, LH))
    vts(ci(1), ci(0), 15, None, AND)
    vts(ci(2), ci(0), 4, 1, SHR, AND)
    vts(ci(3), ci(0), NB - 1, None, AND)
    vcopy(S("col", 1, 3), S("coli", 1, 3))
    vts(col(3), col(2), -4.0, 4.0, ALU.mult, ALU.add)
    vts(col(4), col(2), 4.0, None, ALU.mult)
    for u in range(2):
        act(idn("Ie", u), idn("Id"), ACT.Copy, 0.0, col(3 + u))
        vts(col(15 + u), col(1), float(W + 16 * u), None, ALU.add)
        vcopy(S("rp", u, u + 1), ci(3))
    act(S("Ie12", 0, 256), S("Ie", 0, 256), ACT.Copy, 0.0, 1024.0)
    vset(S("EP", 0, H * EW), 0.0)
    vset(S("NP", 0, H * EW), 0.0)
    vts(col(5), S("Id", 0, 1), 2.0 ** 24, None, ALU.mult)
    vtt(col(6), col(5), S("Id", 1, 2), ALU.subtract)
    vts(S("cap", 0, NB), S("ones", 0, NB), col(6), None, ALU.mult)
    vset(S("cN", 0, 32), FAR)
    vts(col(11), S("thi", 0, 1), -512.0, None, ALU.add)
    vts(col(12), col(11), 32768.0, None, ALU.mult)
    for c in range(4):
        a, b = 512 * c, 512 * c + 512
        vts(S("MT", a, b), S("nmi", a, b), BIG, -BIG, ALU.add, ALU.add)
        vts(S("NI", a, b), S("nmi", a, b), 4095, None, AND)
        act(S("MC", a, b), S("MT", a, b), ACT.Relu, -2.0 ** 29 * (NONE - 1), 2.0 ** 17)
        act(S("NT", a, b), S("NI", a, b), ACT.Copy)
        if c % 2:
            dma("G", S("MT", a - 512, b), S("MC", a - 512, b), 2500, acc=True)
    vset(S("XT", NONE, W), XN)
    if TWO:
        dma("Y", S("ME", 0, W), MTw, 3500)

    ep = lambda n, h: S(n, h * EW + 16, h * EW + 16 + LH)
    row = lambda n, h, r=0, m=1: S(n, (h * REP + r) * LH, (h * REP + r + m) * LH)

    def bcast(ps, src, tag):
        mm([(S(ps, a, 16 * _n(src), 16), idn("Sel", a), src) for a in range(16)], each=1, tag=tag)

    def rows(name, h, src, tag):
        p = reg()
        bcast(p, src, tag)
        for r in range(1 if GREP else REP):
            act(row(name, h, r), S(p, 0, LH), ACT.Copy, 0.0, 4096.0)
        r = 1
        while GREP and r < REP:
            gsel(row(name, h, r, r), row(name, h, 0, r), [[0, r * LH]], ALU.is_ge, 0, 0)
            r *= 2

    def turn(h, pad, tr, off, tf, mask):
        e0, t0, p = h * EW, h * TW, reg()
        vtr(S(tr, t0, t0 + LH), ep(pad, h))
        vtr(S(tr, t0 + LH, t0 + TW), S(pad, e0, e0 + EW))
        src = lambda b, u: t0 + 16 * u + (32 * (b // 2) if b % 2 == u else LH + 32 * ((b + 1) // 2))
        mm([(S(p, b, LH, NB), idn(mask, u), S(tr, src(b, u), src(b, u) + 16)) for b in range(NB) for u in range(2)],
           each=2, tag="t" + off)
        vts(S(off, h * LH, h * LH + LH), S(p, 0, LH), float(NONE), None, ALU.min)
        if GTF:
            gsel(S(tf, h * LH, h * LH + LH), S(off, h * LH, h * LH + LH), [[0, LH]], ALU.is_ge, 0, 0)
        else:
            vcopy(S(tf, h * LH, h * LH + LH), S(off, h * LH, h * LH + LH))

    def compare(h, out, win, off, rw):
        k = 0
        for n in KS:
            d = (16 * h + k) * LH
            vtt(S(out, d, d + n * LH), (win, S(off, h * LH + k * NB, h * LH + (k + n) * NB)), row(rw, h, 0, n),
                ALU.is_equal, tag=out + str(k * NB // 64))
            k += n

    def keys(h, eq, val, sg, tf, kc, run, first, key):
        p, q, n, h0 = reg(), reg(), reg(), h * LH
        low = [(S(p, 0, LH), idn("I11"), S("KC", kc, kc + LH)), (S(p, 0, LH), idn("Id"), S(tf, h0, h0 + LH)),
               (S(p, LH, LH + NB),) + first]
        for c in range(2):
            d0, k0, u = h * 16 * LH + 1024 * c, h0 + 64 * c, val + str(c)
            pc, pk = S(q, 64 * c, 64 * c + 64), S(p, 64 * c, 64 * c + 64)
            mm([(pc, Bw("B1", a), S(eq, d0 + a, d0 + 1024, 16)) for a in range(16)], tag="C" + u)
            if kc == 0:
                mm(low * (1 - c) + [(pk, Bw("B15", a), S(val, d0 + a, d0 + 1024, 16)) for a in range(16)],
                   start=c == 0, stop=False, tag="K" + u)
            else:
                mm([(S(n, 64 * c, 64 * c + 64), Bw("B1", a), S(val, d0 + a, d0 + 1024, 16)) for a in range(16)], tag="K" + u)
        act(S(sg, h0, h0 + LH), S(q, 0, LH), ACT.Sign)
        if kc:
            act(S("CT", h0, h0 + LH), S(n, 0, LH), ACT.Identity, 192.0, -1.0 / 32768)
        pk = S(p, 0, LH)
        mm((low + [(pk, idn("I15"), S("CT", h0, h0 + LH))] if kc else []) + [(pk, idn("IR"), S(sg, h0, h0 + LH))],
           start=kc > 0, tag="L" + val)
        for b in range(NB):
            i, o = S(p, b, LH + NB, NB), S(key, h * NB + b, h * NB + b + 1)
            add("V", 64 * CYC, [i], [o], lambda q, R, i=i, o=o: q.tensor_reduce(R(o), R(i), AxisListType.X, ALU.min), tag=run)

    def scatter(table, o0, a, b, op, tag):
        for k in range(14, -1, -2):
            u = lambda s: S(s, 16 * k, 16 * k + 32) if SCRATCH[s][1][1] > 32 else S(s, 0, 32)
            out = (S(table, 0, WP), S("off", o0 + k, o0 + k + 2))
            if b:
                vtt(out, u(a), u(b), op, tag=tag)
            else:
                vcopy(out, u(a), tag=tag)

    for t in range(RO):
        last = t == RO - 1
        at[1] = t
        WI, ZB, ZO = "WI%d" % t, "ZB%d" % t, "ZO%d" % t
        if last:
            for c in range(0, W, 512):
                vts(S("MC", c, c + 512), S("MT", c, c + 512), TOP, None, ALU.min)
            dma("G", S("MC", 0, W), NTw, 5000, acc=True)
        for h in range(H):
            at[0] = "." + str(h)
            b0, b1, l0, d0 = h * NB, h * NB + NB, h * LH, h * 16 * LH
            zb, wi = S(ZB, l0, l0 + LH), S(WI, b0, b1)
            vcopy(S("wu", b0, b1), wi)
            vts(S("LST", 16 + b0, 16 + b1), wi, 1.0 / 4096, None, ALU.mult, tag="ws")
            if t:
                act(ep("EP", h), (S("ME", 0, W) if TWO else MTw, S("wu", b0, b1)), ACT.Copy, 0.0, 2.0 ** -14)
            else:
                vts(S("E0", l0, l0 + LH), (S("nmi", 0, W), S("wu", b0, b1)), 12, None, SHR)
                vts(ep("EP", h), S("E0", l0, l0 + LH), 0.25, None, ALU.mult)
            turn(h, "EP", "TE", "eoff", "ETf", "Ie")
            rows("WR", h, S("LST", 16 + b0, 16 + b1), "bw")
            compare(h, "EQN", NTw if t else S("NI", 0, W), "eoff", "WR")
            kp, c0 = 512 // LH, 0
            for c in range(16 // kp):
                xg, ad = S("XG", d0 + 512 * c, d0 + 512 * c + 512), S("AD", d0 + 512 * c, d0 + 512 * c + 512)
                if c in XV[h]:
                    for k in range(kp):
                        o0 = l0 + (c * kp + k) * NB
                        vtt(S("XG", xg[1] + k * LH, xg[1] + k * LH + LH), (XTw, S("eoff", o0, o0 + NB)), zb, ALU.subtract, tag="xV")
                    act(ad, xg, ACT.Abs, tag="AD%d" % c)
                    continue
                if c >= c0:
                    c0 = c + 1
                    while c0 < 16 // kp and c0 - c < XS and c0 not in XV[h]:
                        c0 += 1
                    act(S("XG", xg[1], d0 + 512 * c0), (XTw, S("eoff", l0 + 32 * c, l0 + 32 * c0)), ACT.Copy, tag="xS%d" % c)
                p = reg()
                mm([(S(p, 0, 512), idn("Id"), xg)] + [(S(p, k * LH, k * LH + LH), idn("nId"), zb) for k in range(kp)], tag="xP")
                act(ad, S(p, 0, 512), ACT.Abs, tag="AD%d" % c)
            keys(h, "EQN", "AD", "SG", "ETf", 0, "RUN", (idn("ones"), S("cap", 0, NB)), "KEY")
            vts(S("oi", b0, b1), S("KEY", b0, b1), NONE, None, AND)
            vcopy(S("ou", b0, b1), S("oi", b0, b1))
            vts(S("LST", b0, b1), S("oi", b0, b1), 0.25, None, ALU.mult, tag="ol")
            act(S("o4", 32 * h, 32 * h + 32), (S("oi", b0, b1), S("rp", 0, 2)), ACT.Copy, 0.0, 0.25)
            if t == 0:
                act(ep("EP", h), (MTw, S("wu", b0, b1)), ACT.Copy, 0.0, 2.0 ** -14, tag="EQ")
        at[0] = ""
        if last:
            vset(S("XT", NONE, W), 255.0)
        for h in range(H):
            at[0] = "." + str(h)
            b0, b1, l0, d0 = h * NB, h * NB + NB, h * LH, h * 16 * LH
            zo = S(ZO, l0, l0 + LH)
            act(ep("NP", h), (NTw, S("ou", b0, b1)), ACT.Copy, 0.0, 1.0 / 4096)
            turn(h, "NP", "TN", "uoff", "UTf", "Ie12")
            po = reg()
            bcast(po, S("o4", 32 * h, 32 * h + 32), "bo")
            act(S("OR", l0, l0 + LH), S(po, 0, LH), ACT.Copy, 0.0, 4096.0)
            if last:
                act(zo, (XTw, S("ou", b0, b1)), ACT.Copy, tag="xo")
            else:
                vts(zo, (XTw, S("ou", b0, b1)), ZP, None, ALU.min, tag="xo")
            if h == H - 1:
                send(S("ZF" if last else "ZB%d" % (t + 1), 0, 256), S(ZO, 0, 256), 256 * 256)
            for c in range(0, 4, MS):
                act(S("MG", d0 + 512 * c, d0 + 512 * (c + MS)), (MTw, S("uoff", l0 + 32 * c, l0 + 32 * (c + MS))),
                    ACT.Copy, 0.0, 2.0 ** -14, tag="MG%d" % (c // 2))
            for c in range(4):
                d = d0 + 512 * c
                vtt(S("EQM", d, d + 512), S("MG", d, d + 512), S(po, 0, 512), ALU.is_equal, tag="EQM%d" % (c // 2))
            keys(h, "EQM", "MG", "SG2", "UTf", LH, "RUN2", (idn("I12"), S("LST", 16 + b0, 16 + b1)), "KEY2")
            if last:
                vts(S("wand", b0, b1), S("KEY2", b0, b1), NONE, None, AND)
                vcopy(S("WOF", b0, b1), S("wand", b0, b1))
                send(S("WF", b0, b1), S("WOF", b0, b1), 512 * NB)
            else:
                vts(S("WO%d" % t, b0, b1), S("KEY2", b0, b1), NONE, None, AND, tag="wand")
                send(S("WI%d" % (t + 1), b0, b1), S("WO%d" % t, b0, b1), 512 * NB)
        at[0] = ""
        fail, FR = lst(4), S("FR", 0, 256)
        vts(fail, S("KEY", 0, 16), col(12), -4096.0, ALU.is_ge, ALU.mult, tag="fail")
        vts(lst(6), S("oi", 0, 16), float(NONE), None, ALU.is_equal, tag="FL")
        vtt(lst(5), lst(1), fail, ALU.mult, tag="fw")
        rw2 = lambda u, h: row("WR", h) if u else S("OR", h * LH, h * LH + LH)
        pd, pr = reg(), S(reg(), 0, 32)
        mm([(S(pd, a, 512, 16), idn("I12"), lst(0, 2)) for a in range(16)], each=1, tag="pd")
        for u, rw in enumerate(("OR", "WR")):
            for h in range(H):
                c, r = 256 * u + h * LH, rw2(u, h)
                vtt(S("EQ", c, c + LH), S(pd, c, c + LH), r, ALU.is_equal)
                vtt(S("EQ", 512 + c + 16, 512 + c + LH), S(pd, c, c + LH - 16), S(rw, r[1] + 16, r[2]), ALU.is_equal)
        mm([(pr, S("Bt", 143 * a + 15, 143 * a + 143), S("EQ", a, 512, 16)) for a in range(16)]
           + [(S(pr[0], 1, 32, 2), Bw("B1", a), S("EQ", 528 + a, 1024, 32)) for a in range(16)]
           + [(S(pr[0], 0, 16), idn("Im10"), lst(0)), (S(pr[0], 16, 32), idn("Id"), lst(1)),
              (S(pr[0], 0, 16), idn("Id"), lst(6))], tag="pr")
        for u in range(2):
            vts(S("off", u, 32, 2), S(pr[0], u, 32, 2), 4096.0, col(15 + u), ALU.mult, ALU.min)
        neM, neN = S("NE", 0, 256), S("NE", 256, 512)
        p = reg()
        for u in range(2):
            vtt(lst(2 + u), lst(u), fail, ALU.add, tag="op")
        bcast(p, lst(2, 2), "bp")
        act(FR, S(p, 256, 512), ACT.Relu, 0.0, -2.0 / 4096)
        for u, pad in enumerate(("EP", "NP")):
            for h in range(H):
                c = 256 * u + h * LH
                vtt(S("NE", c, c + LH), ep(pad, h), S(p, c, c + LH), ALU.not_equal)
        entries = lambda p, pad: [(S(p, h * LH, h * LH + LH), idn("I12"), ep(pad, h)) for h in range(H)]
        Pm = lambda a: S("Bm", 144 * a + 15 - (a + t) % 16, 144 * a + 143 - (a + t) % 16)
        p = reg()
        pA, pB = S(p, 0, 256), S(p, 256, 512)
        if last:
            act(S("Mo", 0, 256), (MTw, S("ou", 0, 16)), ACT.Relu, TOP, -1.0)
        mm([(pA, idn("I11"), FR), (pB, idn("Hn"), FR)] + entries(p, "NP") + [(pB, idn("If"), S("Mo", 0, 256))] * last
           + [(S(p, a, 512, 16), Pm(a), lst(4, 2)) for a in range(16)], stop=False, tag="pN")
        mm([(pA, idn("nI12"), neN), (pB, idn("H47"), neN)], start=False, tag="qN")
        act(S("nA", 0, 256), pA, ACT.Relu)
        act(S("nB", 0, 256), pB, ACT.Identity, TOP * last, -1.0)
        scatter("MC" if last else "NT", 0, "nA", "nB", ALU.add, "scN")
        p = S(reg(), 0, 256)
        mm([(p, idn("I27" if last else "nI27"), FR)] + entries(p[0], "EP") + [(p, idn("nI28" if last else "I28"), neM)], tag="pM")
        if last:
            act(S("rM", 0, 256), p, ACT.Relu, TOP - 2.0 ** 30, -4.0)
            act(S("Yw", 0, 256), (S("MC", 0, W), S("wu", 0, 16)), ACT.Copy)
            scatter("MC", 16, "Yw", "rM", ALU.add, "scM")
        else:
            act(S("rM", 0, 256), p, ACT.Relu, FAR, -4.0)
            if TWO:
                scatter("ME", 16, "cN", "rM", ALU.subtract, "scE")
            scatter("MT", 16, "cN", "rM", ALU.subtract, "scM")
            p = reg()
            mm([(S(p, 256 * u, 256 * u + 256), idn(n), s) for u in range(2)
                for n, s in (("Id", S(ZO, 0, 256)), ("nId" if u else "Id", FR))], each=2, tag="pX")
            vtt(S("x1", 0, 256), S(ZB, 0, 256), S(p, 0, 256), ALU.min)
            vtt(S("x2", 0, 256), S("x1", 0, 256), S(p, 256, 512), ALU.max)
            scatter("XT", 0, "x2", None, None, "scX")
            p = S(reg(), 0, 16)
            mm([(p, idn("ones"), fail)], tag="pS")
            add("V", 64 * CYC, [p], [col(13)],
                lambda q, R, p=p: q.tensor_reduce(R(col(13)), R(p), AxisListType.X, ALU.add, negate=True), tag="s")
            vts(ci(13), col(13), -1.0 / 4096, None, ALU.mult, tag="s")
            vts(ci(14), ci(13), 31, None, AND, tag="s")
            vts(col(12), ci(14), col(11), 32768.0, ALU.add, ALU.mult, tag="s")
    dma("Y", S("ynm", 0, 0), S("MC", 0, W), 3500)
    dma("Y", S("yz", 0, 0), S("ZF", 0, 256), 300)
    dma("Y", S("yw", 0, 0), S("WF", 0, 16), 100)
    return ops


def find_deps(ops):
    hist = {}
    for i, o in enumerate(ops):
        d = {i - 1} if 0 < i < NL else set()
        acc = [(s, False) for s in o["rd"]] + [(s, True) for s in o["wr"]] + ([(o["dst"], True)] if "dst" in o else [])
        acc = [(s[0], s[0][0] == "@", w) + ((0, 1 << 20) if s[0][0] == "@" or s[2] == 0 else (s[1], s[2])) for s, w in acc]
        for name, psum, w, lo, hi in acc:
            for j, a, b, pw in hist.get(name, []):
                if j != i and b > lo and hi > a and (pw or w or (psum and ops[j]["eng"] != o["eng"])):
                    d.add(j)
        for name, psum, w, lo, hi in acc:
            l = hist.setdefault(name, [])
            if w and not psum:
                l[:] = [e for e in l if e[0] == i or not (lo <= e[1] and e[2] <= hi)]
            l.append((i, lo, hi, w))
        o["deps"] = sorted(d)
        o["wait"] = [j for j in o["deps"] if i >= NL and (ops[j]["eng"] != "P" or o["eng"] != "P")]
        o["regs"] = sorted(set(s[0] for s in o["rd"] + o["wr"] if s[0][0] == "@"))
        o["succ"] = []
        for j in o["deps"]:
            ops[j]["succ"].append(i)


def costs(ops, gath, scat, pcyc):
    return [o["fix"] * pcyc if o["eng"] == "P" else o["fix"] + CYC * (gath * o["ge"] + scat * o["se"]) for o in ops]


def pick(ready, free, rt, prio, look, later):
    best = None
    for e in "VSPGY":
        cand = [(max(rt[i], free[e], later(i)), i) for i in ready[e]]
        if cand:
            t0 = min(cand)[0] + look
            c = max([c for c in cand if c[0] <= t0], key=lambda c: (prio[c[1]], -c[1]))
            if best is None or c[0] < best[0]:
                best = c
    return best


def schedule(ops, cost, prio, look, hop):
    n = len(ops)
    users = {}
    for o in ops:
        for r in o["regs"]:
            users[r] = users.get(r, 0) + 1
    left = [len(o["deps"]) for o in ops]
    ready = {e: [i for i in range(n) if left[i] == 0 and ops[i]["eng"] == e] for e in "VSPGY"}
    free = {e: 0.0 for e in "VSPGY"}
    fin, rt = [0.0] * n, [0.0] * n
    bank, lastuse, held, rel, order, extra = {}, [[] for _ in range(8)], [False] * 8, [0.0] * 8, [], {}
    while len(order) < n:
        fb = min([(rel[b], b) for b in range(8) if not held[b]] + [(1e18, -1)])
        st, i = pick(ready, free, rt, prio, look, lambda i: fb[0] if ops[i]["regs"] and ops[i]["regs"][0] not in bank else 0.0)
        if st >= 1e17:
            return None
        o = ops[i]
        if o["regs"] and o["regs"][0] not in bank:
            bank[o["regs"][0]] = fb[1]
            extra[i], lastuse[fb[1]] = [j for j in lastuse[fb[1]] if ops[j]["eng"] != "P"], []
        free[o["eng"]] = st + cost[i]
        fin[i] = st + cost[i] + o["lat"]
        for r in o["regs"]:
            users[r] -= 1
            lastuse[bank[r]].append(i)
            rel[bank[r]] = max(rel[bank[r]], fin[i] + hop)
            held[bank[r]] = users[r] > 0
        order.append(i)
        ready[o["eng"]].remove(i)
        for k in o["succ"]:
            left[k] -= 1
            if left[k] == 0:
                rt[k] = max([fin[j] + hop for j in ops[k]["wait"]] + [0.0])
                ready[ops[k]["eng"]].append(k)
    return order, bank, extra, fin


def backward(ops, cost, prio, look, hop):
    n = len(ops)
    left = [len(o["succ"]) for o in ops]
    ready = {e: [i for i in range(n) if left[i] == 0 and ops[i]["eng"] == e] for e in "VSPGY"}
    free = {e: 0.0 for e in "VSPGY"}
    rt, end = [o["lat"] for o in ops], [0.0] * n
    for _ in range(n):
        st, i = pick(ready, free, rt, prio, look, lambda i: 0.0)
        o = ops[i]
        end[i] = free[o["eng"]] = st + cost[i]
        ready[o["eng"]].remove(i)
        for j in o["deps"]:
            left[j] -= 1
            rt[j] = max(rt[j], end[i] + (hop + ops[j]["lat"] if j in o["wait"] else 0))
            if left[j] == 0:
                ready[ops[j]["eng"]].append(j)
    return end


def replay(ops, plan, cost, hop):
    free, fin = {}, {}
    for i in plan[0]:
        o = ops[i]
        st = max([free.get(o["eng"], 0.0)] + [fin[j] + hop for j in o["wait"] + plan[2].get(i, [])])
        free[o["eng"]] = st + cost[i]
        fin[i] = st + cost[i] + o["lat"]
    return max(fin.values())


def best_plan(ops, tries):
    cs = [costs(ops, *s[:3]) for s in SPEEDS]
    c, hop, seed = cs[0], SPEEDS[0][3], [1]

    def rnd(k):
        seed[0] = (seed[0] * 1103515245 + 12345) % (1 << 31)
        return (seed[0] >> 8) % k

    def value(p):
        return sum(w * replay(ops, p, x, s[3]) for w, x, s in zip((2.0, 1.1, 0.85, 0.8), cs, SPEEDS))
    prio = [0.0] * len(ops)
    for i in range(len(ops) - 1, -1, -1):
        prio[i] = c[i] + ops[i]["lat"] + hop + max([prio[k] for k in ops[i]["succ"]] + [0.0])
    early = "fail FL op wp fw bf FR pd EQ pr off bp NE pN nA nB pM rM pX x1 x2".split()
    best = schedule(ops, c, [p + 3000 * (o["tag"][-2:] == ".0" or o["tag"] in early) for p, o in zip(prio, ops)], 0, hop)
    bv, tags = value(best), sorted(set(o["tag"] for o in ops))
    for it in range(tries):
        look = (0, 0, 20, 50)[rnd(4)]
        if rnd(3) == 0:
            e = backward(ops, c, [x + rnd(300) - 150 for x in best[3]], look, hop)
        else:
            e = [y + o["lat"] - x for x, y, o in zip(best[3], c, ops)]
        t = rnd(5)
        b = {tags[rnd(len(tags))]: (-3000, -1000, -500, -200, 200, 500, 1000, 3000)[rnd(8)] for _ in range((1, 2, 4)[rnd(3)])}
        if rnd(2):
            e = [x + (b.get(o["tag"], 0) if t > 2 or o["t"] == t else 0) for x, o in zip(e, ops)]
        if rnd(2):
            i, way, far, d = rnd(len(ops)), ("deps", "succ")[rnd(2)], (1500, 3000, 6000)[rnd(3)], (300, 1000, 2500)[rnd(3)]
            cone, todo = {i}, [i]
            while todo:
                for j in ops[todo.pop()][way]:
                    if j not in cone and abs(best[3][j] - best[3][i]) < far:
                        cone.add(j)
                        todo.append(j)
            for j in cone:
                e[j] += d if way == "deps" else -d
        p = schedule(ops, c, e, look, hop)
        if p:
            v = value(p)
            if v < bv + 1500.0 * max(0.0, 1 - it / (0.8 * tries)) * (rnd(1000) / 1000.0) ** 3:
                best, bv = p, v
    for e in range(TURNS):
        best = refine(ops, banks(ops, best), rnd, MOVES // TURNS, HEAT * (1 - e / TURNS), HEAT * (1 - (e + 1) / TURNS))
    return best


def polish(ops, order, rnd, moves):
    n = len(ops)
    eng = ["VSPGY".index(o["eng"]) for o in ops]
    wait, deps, succ = [o["wait"] for o in ops], [o["deps"] for o in ops], [o["succ"] for o in ops]
    regs = [o["regs"][0] if o["regs"] else None for o in ops]
    total = {}
    for r in regs:
        total[r] = total.get(r, 0) + 1
    sets = [(costs(ops, *s[:3]), [o["lat"] * f + s[3] for o in ops], w) for s, w, f in zip(SPEEDS, WEIGHTS, LATS) if w]

    def run(order, cost, lat, extra):
        free, fin, why, prev = [0.0] * 5, [0.0] * n, [-1] * n, [-1] * 5
        first = extra is None
        if first:
            extra, bank, left, held, rel, use = {}, {}, dict(total), [False] * 8, [0.0] * 8, [[] for _ in range(8)]
        for i in order:
            e = eng[i]
            st, y = free[e], prev[e]
            for j in wait[i]:
                if fin[j] > st:
                    st, y = fin[j], j
            r = regs[i]
            if r:
                if first:
                    if r not in bank:
                        b = min([(rel[k], k) for k in range(8) if not held[k]] + [(0, -1)] * all(held))[1]
                        if b < 0:
                            return None
                        bank[r], extra[i], use[b] = b, [j for j in use[b] if eng[j] != 2], []
                    b = bank[r]
                    left[r] -= 1
                    held[b] = left[r] > 0
                    use[b].append(i)
                for j in extra.get(i, ()):
                    if fin[j] > st:
                        st, y = fin[j], j
            free[e] = st = st + cost[i]
            fin[i] = st + lat[i]
            if r and first:
                rel[b] = max(rel[b], fin[i])
            why[i], prev[e] = y, i
        return max(fin), fin, why, extra, bank if first else None

    def value(order):
        res = [run(order, sets[0][0], sets[0][1], None)]
        if res[0] is None:
            return None
        res += [run(order, c, l, res[0][3]) for c, l, w in sets[1:]]
        return sum(r[0] * s[2] for r, s in zip(res, sets)), res

    seen, kin = {}, {}
    for i, o in enumerate(ops):
        k = (o["tag"], o["eng"], o["t"])
        seen[k] = seen.get(k, 0) + 1
        kin.setdefault((o["tag"], o["eng"], seen[k]), []).append(i)
    twins = {i: l for l in kin.values() for i in l}
    cur = value(order)
    best = (cur[0], order, cur[1])
    for it in range(moves):
        fin, why = cur[1][rnd(len(sets))][1:3]
        i, path = fin.index(max(fin)), []
        while why[i] >= 0:
            if eng[why[i]] == eng[i] and why[i] not in deps[i]:
                path.append(i)
            i = why[i]
        i = path[rnd(len(path))] if path and rnd(6) else rnd(n)
        fwd = rnd(2)
        if rnd(2):
            key = [f - c - l for f, c, l in zip(cur[1][0][1], sets[0][0], sets[0][1])]
            i = i if fwd or why[i] < 0 else why[i]
            far, d = (0, 700, 2000, 5000)[rnd(4)], (120, 300, 700, 1500, 3000)[rnd(5)]
            todo = list(twins[i]) if rnd(2) else [i]
            cone = {k: key[k] for k in todo}
            while todo:
                k = todo.pop()
                for j in (deps if fwd else succ)[k]:
                    if j not in cone and abs(key[j] - cone[k]) < far:
                        cone[j] = cone[k]
                        todo.append(j)
            for k in cone:
                key[k] += -d if fwd else d
            for k in range(n):
                for j in deps[k]:
                    if key[j] >= key[k]:
                        key[k] = key[j] + 0.01
            new = sorted(range(n), key=lambda k: key[k])
        else:
            pos = {k: p for p, k in enumerate(order)}
            mine = [k for k in order[max(0, pos[i] - 120):pos[i]] if eng[k] == eng[i]][-(1, 1, 2, 4, 8, 16)[rnd(6)]:]
            if not mine:
                continue
            p = mine[0]
            a, b = pos[p], pos[i]
            cone, todo = {i if fwd else p}, [i if fwd else p]
            while todo:
                for j in (deps if fwd else succ)[todo.pop()]:
                    if j not in cone and a <= pos[j] <= b:
                        cone.add(j)
                        todo.append(j)
            if p in cone and i in cone:
                continue
            one, two = [k for k in order[a:b + 1] if k in cone], [k for k in order[a:b + 1] if k not in cone]
            new = order[:a] + (one + two if fwd else two + one) + order[b + 1:]
        v = value(new)
        if v and v[0] <= cur[0] + HEAT * max(0.0, 1 - it / (0.9 * moves)) * (rnd(1000) / 1000.0) ** 2:
            order, cur = new, v
            if v[0] < best[0]:
                best = (v[0], new, v[1])
    return best[1], best[2][0][4], best[2][0][3], best[2][0][1]


def banks(ops, plan):
    left, bank, rel, held = {}, {}, [0.0] * 8, [False] * 8
    for o in ops:
        for r in o["regs"]:
            left[r] = left.get(r, 0) + 1
    for i in plan[0]:
        for r in ops[i]["regs"]:
            if r not in bank:
                bank[r] = min((held[b], rel[b], b) for b in range(8))[2]
            left[r] -= 1
            held[bank[r]], rel[bank[r]] = left[r] > 0, max(rel[bank[r]], plan[3][i])
    return plan[0], bank


def refine(ops, plan, rnd, moves, hot, cold):
    n, order, bank = len(ops), list(plan[0]), plan[1]
    eng = ["VSPGY".index(o["eng"]) for o in ops]
    sets = [(costs(ops, *s[:3]), [o["lat"] * f + s[3] for o in ops], w) for s, w, f in zip(SPEEDS, WEIGHTS, LATS) if w]
    use, held, deps, wait, extra = {}, {}, [list(o["deps"]) for o in ops], [list(o["wait"]) for o in ops], {}
    for i in order:
        for r in ops[i]["regs"]:
            b = bank[r]
            if held.get(b) != r:
                extra[i] = [j for j in use.get(b, []) if eng[j] != 2]
                deps[i] += use.get(b, [])
                wait[i] += extra[i]
                use[b], held[b] = [], r
            use[b].append(i)
    succ, after = [[] for _ in ops], [[] for _ in ops]
    for i in range(n):
        for j in deps[i]:
            succ[j].append(i)
        for j in wait[i]:
            after[j].append(i)

    def paths(order):
        out = []
        for cost, lat, w in sets:
            free, end, tail, why, prev = [0.0] * 5, [0.0] * n, [0.0] * n, [-1] * n, [-1] * 5
            for i in order:
                e = eng[i]
                st, y = free[e], prev[e]
                for j in wait[i]:
                    if end[j] + lat[j] > st:
                        st, y = end[j] + lat[j], j
                free[e] = end[i] = st + cost[i]
                why[i], prev[e] = y, i
            free = [0.0] * 5
            for i in order[::-1]:
                x = max([tail[k] for k in after[i]] + [0.0]) + lat[i]
                free[eng[i]] = tail[i] = max(x, free[eng[i]]) + cost[i]
            out.append((end, tail, why, max(tail)))
        return out

    def through(win, a, b):
        before, behind, res = {}, {}, []
        for k in range(a - 1, max(-1, a - 200), -1):
            before.setdefault(eng[order[k]], order[k])
            if len(before) > 3:
                break
        for k in range(b + 1, min(n, b + 200)):
            behind.setdefault(eng[order[k]], order[k])
            if len(behind) > 3:
                break
        for (cost, lat, w), (end, tail, why, top) in zip(sets, cur):
            free, new, m = {e: end[k] for e, k in before.items()}, {}, 0.0
            for i in win:
                st = free.get(eng[i], 0.0)
                for j in wait[i]:
                    x = new.get(j, end[j]) + lat[j]
                    if x > st:
                        st = x
                free[eng[i]] = new[i] = st = st + cost[i]
                x = 0.0
                for k in after[i]:
                    if pos[k] > b and tail[k] > x:
                        x = tail[k]
                if st + lat[i] + x > m:
                    m = st + lat[i] + x
            for e, k in behind.items():
                m = max(m, free.get(e, 0.0) + tail[k])
            res.append(m)
        return res

    worth = lambda c: sum(x[3] * s[2] for x, s in zip(c, sets))
    cur = paths(order)
    best, path = (worth(cur), order), None
    for it in range(moves):
        if path is None:
            pos, path = {k: p for p, k in enumerate(order)}, []
            for end, tail, why, top in cur:
                i = end.index(max(end))
                while why[i] >= 0:
                    if eng[why[i]] == eng[i] and why[i] not in deps[i]:
                        path.append(i)
                    i = why[i]
        i = path[rnd(len(path))] if path and rnd(4) else rnd(n)
        mine = [k for k in order[max(0, pos[i] - 90):pos[i]] if eng[k] == eng[i]][-(1, 1, 2, 3, 5, 8, 14)[rnd(7)]:]
        if not mine:
            continue
        p, fwd = mine[0], rnd(2)
        a, b = pos[p], pos[i]
        cone, todo = {i if fwd else p}, [i if fwd else p]
        while todo:
            for j in (deps if fwd else succ)[todo.pop()]:
                if j not in cone and a <= pos[j] <= b:
                    cone.add(j)
                    todo.append(j)
        if p in cone and i in cone:
            continue
        old = order[a:b + 1]
        one, two = [k for k in old if k in cone], [k for k in old if k not in cone]
        win = one + two if fwd else two + one
        d = sum(s[2] * (max(x, c[3] - SLACK) - max(y, c[3] - SLACK))
                for x, y, c, s in zip(through(win, a, b), through(old, a, b), cur, sets))
        if d <= (hot + (cold - hot) * it / moves) * (rnd(1000) / 1000.0) ** 3:
            order = order[:a] + win + order[b + 1:]
            cur, path = paths(order), None
            if rnd(8) == 0:
                order.sort(key=lambda k: cur[0][0][k] - sets[0][0][k])
            if worth(cur) < best[0]:
                best = (worth(cur), order)
    cur = paths(best[1])
    return best[1], bank, extra, [e + l for e, l in zip(cur[0][0], sets[0][1])]


OPS = build_ops()
find_deps(OPS)
PLAN = best_plan(OPS, TRIES)
SEMAPHORES = ["cV", "cS", "cP", "cG", "sent"] + ["d%d" % _i for _i, _o in enumerate(OPS) if _o["kind"] != "c"]


def bits(m):
    return bin(m).count("1")


def rank_program(g, core, T, topo):
    rank = T.rank_of(core)
    if rank is None:
        return
    Q = {"V": g.vector, "S": g.scalar, "P": g.tensor, "G": g, "Y": g.sync}
    order, bank, extra = PLAN[:3]

    def R(s):
        t = T["ps%d" % bank[s[0]]] if s[0][0] == "@" else T[s[0]]
        if s[2] == 0:
            return t[:]
        return t[:, s[1]:s[2]] if s[3] == 1 else t[:, s[1]:s[2]:s[3]]

    cnt = {e: 0 for e in "VSPG"}
    known = {e: {} for e in "VSPGY"}
    mark, clock, place, sent = {}, {}, {i: k for k, i in enumerate(order)}, 0
    for i in order:
        o = OPS[i]
        e = o["eng"]
        kn = known[e]
        for j in sorted(o["wait"] + extra.get(i, []), key=lambda j: -place[j]):
            sem, val = mark[j]
            if kn.get(sem, 0) < val:
                Q[e].wait_ge(T.sem[sem], val)
                kn[sem] = val
                for k, v in clock[j].items():
                    kn[k] = max(kn.get(k, 0), v)
        clock[i] = dict(kn)
        if o["kind"] == "c":
            cnt[e] += 1
            o["fn"](Q[e], R).then_inc(T.sem["c" + e], 1)
            mark[i] = ("c" + e, cnt[e])
        elif o["kind"] == "d":
            o["fn"](Q[e], R).then_inc(T.sem["d%d" % i], 16)
            mark[i] = ("d%d" % i, 16)
        else:
            step = 1 + o["t"] % (NR - 1)
            to, frm = T.cores[(rank + step) % NR], T.cores[(rank - step) % NR]
            rid, pid = topo.addr(to)[:2]
            m = topo.mask(core, to)
            g.remote_dma(R(o["dst"]), R(o["src"]), T.sem["d%d" % i], T.sem.sent, pid, rid, m)
            sent += bits(m)
            mark[i] = ("d%d" % i, bits(topo.mask(frm, core)))
            clock[i] = {}
    for e in "VSPG":
        g.wait_ge(T.sem["c" + e], cnt[e])
    g.wait_ge(T.sem.sent, sent)
    for i, o in enumerate(OPS):
        if o["kind"] != "c":
            g.wait_ge(T.sem[mark[i][0]], mark[i][1])
